import numpy as np
import ml_dtypes


def mxq(x, axis, fmt="e4m3"):
    dtype, down = {"e4m3": (ml_dtypes.float8_e4m3fn, 7), "e5m2": (ml_dtypes.float8_e5m2, 14)}[fmt]
    v = np.moveaxis(np.asarray(x, np.float32).astype(ml_dtypes.bfloat16).astype(np.float64), axis, -1)
    blocks = v.reshape(v.shape[:-1] + (-1, 32))
    amax = np.abs(blocks).max(-1, keepdims=True)
    byte = np.maximum(np.where(amax > 0, np.frexp(amax)[1] - 1 + 127, 0) - down, 1)
    scale = np.exp2(byte - 127.0)
    codes = (blocks / scale).astype(np.float32).astype(dtype).astype(np.float64)
    return np.moveaxis((codes * scale).reshape(v.shape), -1, axis)


WIDE = False


def mx_kscale(k):
    if not WIDE:
        return np.ones(k)
    levels = np.array([10, -10, 5, -5, 0])
    if k % 512:
        return np.exp2(np.random.permutation(np.resize(levels, k // 32))).repeat(32)
    a = np.empty((k // 512, 16))
    for p in range(k // 512):
        a[p, :8] = np.random.permutation(np.resize(levels, 8))
        for g in range(8):
            far = levels[np.abs(levels - a[p, g]) >= 10]
            a[p, g + 8] = far[np.random.randint(len(far))]
    return np.exp2(a.ravel()).repeat(32)


def f64(x):
    return np.asarray(x).astype(np.float64)


def striped(idx):
    return np.tile(idx.reshape(-1, 16).T, (8, 1)).astype(np.uint16)


def unstriped(offs):
    return offs[:16].T.reshape(-1).astype(np.int64)


E2M1 = np.array([0.0, 0.5, 1.0, 1.5, 2.0, 3.0, 4.0, 6.0, -0.0, -0.5, -1.0, -1.5, -2.0, -3.0, -4.0, -6.0])


def pack_weight(w, fmt):
    k, n = w.shape
    w = f64(np.asarray(w, np.float32).astype(ml_dtypes.bfloat16)).reshape(k // 32, 32, n)
    amax = np.abs(w).max(1)
    if fmt == "e4m3":
        byte = np.frexp(amax)[1] - 1 + 127 - 7
    else:
        mant, ex = np.frexp(amax / 6.0)
        byte = np.where(mant > 0.5, ex, ex - 1) + 127
    byte = np.clip(np.where(amax > 0, byte, 1), 1, 254)
    scaled = (w * np.exp2(127.0 - byte)[:, None, :]).reshape(k, n).astype(np.float32)
    by_word = np.ascontiguousarray(scaled.reshape(k // 512, 128, 4, n).transpose(0, 1, 3, 2))
    if fmt == "e4m3":
        words = by_word.astype(ml_dtypes.float8_e4m3fn).view(np.uint8)
    else:
        c = by_word.astype(ml_dtypes.float4_e2m1fn).view(np.uint8) & 0xF
        words = (c[..., 0::2] | (c[..., 1::2] << 4)).reshape(k // 512, 128, 2 * n)
    return np.ascontiguousarray(words), np.ascontiguousarray(byte.astype(np.uint8).reshape(k // 512, 16, n))


def unpack_weight(words, scales, fmt):
    g, _, n = scales.shape
    words = np.ascontiguousarray(words).reshape(g, 128, n, -1)
    if fmt == "e4m3":
        vals = words.view(ml_dtypes.float8_e4m3fn).astype(np.float64)
    else:
        nib = np.empty((g, 128, n, 4), np.uint8)
        nib[..., 0::2] = words & 0xF
        nib[..., 1::2] = words >> 4
        vals = E2M1[nib]
    vals = vals * np.repeat(np.exp2(scales.astype(np.float64) - 127.0), 8, axis=1)[..., None]
    return vals.transpose(0, 1, 3, 2).reshape(g * 512, n)


K, T, E, C, H, N = 512, 512, 16, 128, 512, 128


def by_expert(wq, xq):
    return np.concatenate([wq[e].T @ xq[:, e * C:(e + 1) * C] for e in range(E)], axis=1)


def setup_inputs():
    n = np.random.standard_normal
    s = mx_kscale(K)
    u = mx_kscale(H)
    slot_token = np.concatenate([np.random.permutation(T)[:C] for e in range(E)])
    x = pack_weight(n((K, T)) * s[:, None], "e4m3")
    w = [pack_weight(m, "e2m1") for m in n((E, K, N)) / np.sqrt(K) / s[None, :, None]]
    wb = [pack_weight(m, "e4m3") for m in n((E, H, N)) / np.sqrt(H) / u[None, :, None]]
    return {
        "x_words": x[0],
        "x_scales": x[1],
        "w_words": np.stack([m[0] for m in w]),
        "w_scales": np.stack([m[1] for m in w]),
        "wa": (n((E, K, H)) / np.sqrt(K) / s[None, :, None] * u).astype(np.float32),
        "wb_words": np.stack([m[0] for m in wb]),
        "wb_scales": np.stack([m[1] for m in wb]),
        "offs": striped(slot_token),
    }


def reference(x_words, x_scales, w_words, w_scales, wa, wb_words, wb_scales, offs):
    w = np.stack([unpack_weight(w_words[e], w_scales[e], "e2m1") for e in range(E)])
    waq = mxq(f64(wa), 1, "e4m3")
    wb = np.stack([unpack_weight(wb_words[e], wb_scales[e], "e4m3") for e in range(E)])
    idx = unstriped(offs)
    xq = unpack_weight(x_words, x_scales, "e4m3")[:, idx]
    h = by_expert(waq, xq)
    y = by_expert(w, xq) + by_expert(wb, mxq(h, 0, "e4m3"))
    out = y
    return out

@@ -1,0 +1,153 @@
+from contextlib import ExitStack
+
+import concourse.mybir as mybir
+
+K, T, E, C, H, N = 512, 512, 16, 128, 512, 128
+FLOPS = 2 * E * C * (K * H + K * N + H * N)
+
+F32 = mybir.dt.float32
+BF16 = mybir.dt.bfloat16
+I32 = mybir.dt.int32
+U32 = mybir.dt.uint32
+U16 = mybir.dt.uint16
+U8 = mybir.dt.uint8
+FP8X4 = mybir.dt.float8_e4m3fn_x4
+FP4X4 = mybir.dt.float4_e2m1fn_x4
+
+P = 128
+PACK = 4
+GROUP = 4
+GATHER = 256
+VECTOR_M = 76
+LAST_VECTOR_M = 84
+RAW_BYTES = PACK * H * 4
+ROW_BYTES = H * 4
+SCALAR_ALONE = 3
+
+
+def tile_moe_elr_s_none_kernel(tc, x_words, x_scales, w_words, w_scales, wa, wb_words, wb_scales, offs, out):
+    nc = tc.nc
+    with ExitStack() as ctx:
+        keep = ctx.enter_context(tc.tile_pool(name="keep", bufs=1))
+        ring = ctx.enter_context(tc.tile_pool(name="ring", bufs=6))
+        stage = ctx.enter_context(tc.tile_pool(name="stage", bufs=1))
+        psum = ctx.enter_context(tc.psum_pool(name="psum", bufs=4))
+
+        offsets = keep.tile([P, E * C // 16], U16, name="offsets")
+        x_table = keep.tile([P, T], I32, name="x_table", align_bytes=64)
+        x_plane = keep.tile([P, T], U8, name="x_plane", align_bytes=64)
+        w_plane = keep.tile([P, E, N], U8, name="w_plane", align_bytes=64)
+        wb_plane = keep.tile([P, E, N], U8, name="wb_plane", align_bytes=64)
+        for plane in (x_plane, w_plane, wb_plane):
+            nc.vector.memset(plane[:].bitcast(I32), 0)
+
+        raw = [stage.tile([P, PACK, H], F32, name="raw%d" % e, align_bytes=64, offset=e * RAW_BYTES) for e in range(E)]
+        w_codes = [keep.tile([P, GROUP, 2 * N], U8, name="w_codes%d" % g, align_bytes=64) for g in range(E // GROUP)]
+        wb_codes = [keep.tile([P, GROUP, PACK * N], U8, name="wb_codes%d" % g, align_bytes=64) for g in range(E // GROUP)]
+
+        def load_wa(e):
+            nc.sync.dma_start(out=raw[e][:], in_=wa[e].rearrange("(p j) c -> p j c", j=PACK))
+
+        def load_group(g):
+            es = slice(g * GROUP, (g + 1) * GROUP)
+            nc.sync.dma_start(out=w_codes[g][:].bitcast(I32), in_=w_words[es, 0].rearrange("e p b -> p e b").bitcast(I32))
+            nc.sync.dma_start(out=wb_codes[g][:].bitcast(I32), in_=wb_words[es, 0].rearrange("e p n d -> p e (n d)").bitcast(I32))
+
+        nc.sync.dma_start(offsets[:], offs)
+        nc.sync.dma_start(out=x_table[:], in_=x_words[0].rearrange("p t d -> p (t d)").bitcast(I32))
+        load_wa(0)
+        x_rows = x_scales[0].rearrange("(q r) t -> r q t", r=4)
+        w_rows = w_scales[:, 0].rearrange("e (q r) n -> r q e n", r=4)
+        wb_rows = wb_scales[:, 0].rearrange("e (q r) n -> r q e n", r=4)
+        for r in range(4):
+            nc.sync.dma_start(out=x_plane[r:P:32, :].bitcast(I32), in_=x_rows[r].bitcast(I32))
+        for e in range(1, E):
+            load_wa(e)
+            if e <= 4:
+                r = e - 1
+                nc.sync.dma_start(out=w_plane[r:P:32, :, :].bitcast(I32), in_=w_rows[r].bitcast(I32))
+                nc.sync.dma_start(out=wb_plane[r:P:32, :, :].bitcast(I32), in_=wb_rows[r].bitcast(I32))
+            if e % GROUP == GROUP - 1:
+                load_group(e // GROUP)
+
+        slot_words = keep.tile([P, E * C], U32, name="slot_words", align_bytes=64)
+        slot_plane = keep.tile([P, E * C], U8, name="slot_plane", align_bytes=64)
+        for s0 in range(0, E * C, GATHER):
+            piece = offsets[:, s0 // 16 : (s0 + GATHER) // 16]
+            nc.vector.tensor_copy(slot_words[:, s0 : s0 + GATHER], x_table[:].bitcast(U32).indirect(piece))
+            nc.vector.tensor_copy(slot_plane[:, s0 : s0 + GATHER], x_plane[:].indirect(piece))
+
+        wa_codes, wa_plane, h_bf16, h_codes, h_plane = {}, {}, {}, {}, {}
+        grouped = {}
+
+        def round_wa(e):
+            grouped[e] = ring.tile([P, PACK, P, PACK], BF16, name="grouped", align_bytes=64)
+            src = raw[e][:].rearrange("p j (m t) -> p m j t", t=PACK)
+            dst = grouped[e][:].rearrange("p t m j -> p m j t")
+            cut = 0 if e < SCALAR_ALONE else LAST_VECTOR_M if e == E - 1 else VECTOR_M
+            if cut:
+                nc.vector.tensor_copy(out=dst[:, :cut], in_=src[:, :cut])
+            nc.scalar.copy(out=dst[:, cut:], in_=src[:, cut:])
+
+        def quantize_wa(e):
+            wa_codes[e] = ring.tile([P, H], U32, name="wa_codes", align_bytes=64)
+            wa_plane[e] = ring.tile([P, H], U8, name="wa_plane", align_bytes=64)
+            nc.vector.quantize_mx(out=wa_codes[e][:].bitcast(FP8X4), scales=wa_plane[e][:],
+                                  in_=grouped[e][:].rearrange("p t m j -> p (t m j)"))
+
+        def first_product(e):
+            slots = slice(e * C, (e + 1) * C)
+            h_bank = psum.tile([P, PACK, C], F32, name="h_bank")
+            for t in range(PACK):
+                cols = slice(t * P, (t + 1) * P)
+                nc.tensor.matmul_mx(out=h_bank[:, t, :], lhsT=wa_codes[e][:, cols].bitcast(FP8X4), lhsT_scale=wa_plane[e][:, cols],
+                                    rhs=slot_words[:, slots].bitcast(FP8X4), rhs_scale=slot_plane[:, slots], start=True, stop=True)
+            behind = max(e + 1, SCALAR_ALONE)
+            h_bf16[e] = stage.tile([P, C, PACK], BF16, name="h_bf16_%d" % e, align_bytes=64,
+                                   offset=behind * RAW_BYTES + (behind - 1 - e) * ROW_BYTES)
+            nc.scalar.copy(out=h_bf16[e][:], in_=h_bank[:].rearrange("p t n -> p n t"))
+
+        def quantize_h(e):
+            h_codes[e] = keep.tile([P, C], U32, name="h_codes%d" % e, align_bytes=64)
+            h_plane[e] = keep.tile([P, C], U8, name="h_plane%d" % e, align_bytes=64)
+            nc.vector.quantize_mx(out=h_codes[e][:].bitcast(FP8X4), scales=h_plane[e][:],
+                                  in_=h_bf16[e][:].rearrange("p n t -> p (n t)"))
+
+        def second_product(first, count):
+            y_bank = psum.tile([P, count, C], F32, name="y_bank")
+            for u in range(count):
+                e = first + u
+                slots = slice(e * C, (e + 1) * C)
+                g, a = divmod(e, GROUP)
+                nc.tensor.matmul_mx(out=y_bank[:, u, :], lhsT=w_codes[g][:, a, :].bitcast(FP4X4), lhsT_scale=w_plane[:, e, :],
+                                    rhs=slot_words[:, slots].bitcast(FP8X4), rhs_scale=slot_plane[:, slots], start=True, stop=False)
+                nc.tensor.matmul_mx(out=y_bank[:, u, :], lhsT=wb_codes[g][:, a, :].bitcast(FP8X4), lhsT_scale=wb_plane[:, e, :],
+                                    rhs=h_codes[e][:].bitcast(FP8X4), rhs_scale=h_plane[e][:], start=False, stop=True)
+            return y_bank[:].rearrange("p u n -> p (u n)")
+
+        def leave(first, banks, behind, copy):
+            widths = [bank.shape[1] for bank in banks]
+            y = stage.tile([P, sum(widths)], F32, name="y%d" % first, align_bytes=64, offset=behind * RAW_BYTES + ROW_BYTES)
+            for b, bank in enumerate(banks):
+                copy(out=y[:, sum(widths[:b]) : sum(widths[: b + 1])], in_=bank)
+            nc.sync.dma_start(out=out[:, first * C : first * C + sum(widths)], in_=y[:])
+
+        y_banks = []
+        for e in range(SCALAR_ALONE):
+            round_wa(e)
+            quantize_wa(e)
+        for i in range(SCALAR_ALONE, E + 1):
+            if i < E:
+                round_wa(i)
+                quantize_wa(i)
+            for e in range(i) if i == SCALAR_ALONE else [i - 1]:
+                first_product(e)
+                quantize_h(e)
+            if i in (5, 9, 13):
+                y_banks.append(second_product(i - 5, GROUP))
+            if i == 11:
+                leave(0, y_banks[:2], i, nc.scalar.copy)
+            if i == 13:
+                leave(8, y_banks[2:], i, nc.scalar.copy)
+        leave(12, [second_product(12, 3)], 14, nc.vector.tensor_copy)
+        leave(15, [second_product(15, 1)], 16, nc.scalar.copy)

@@ -16,13 +16,16 @@ FP4X4 = mybir.dt.float4_e2m1fn_x4
 
 P = 128
 PACK = 4
+HALF = PACK // 2
 GROUP = 4
 GATHER = 256
-VECTOR_M = 76
-LAST_VECTOR_M = 84
+VECTOR_M = 24
+LAST_VECTOR_M = 16
 RAW_BYTES = PACK * H * 4
 ROW_BYTES = H * 4
 SCALAR_ALONE = 3
+EARLY = 12
+LOADS = [(0, 1), (1, 1), (2, 1), (3, 1), (4, 1), (5, 1), (6, 1), (7, 1), (8, 1), (9, 1), (10, 1), (11, 1), (12, 1), (13, 1), (14, 1), (15, 1)]
 
 
 def tile_moe_elr_s_none_kernel(tc, x_words, x_scales, w_words, w_scales, wa, wb_words, wb_scales, offs, out):
@@ -41,34 +44,41 @@ def tile_moe_elr_s_none_kernel(tc, x_words, x_scales, w_words, w_scales, wa, wb_
         for plane in (x_plane, w_plane, wb_plane):
             nc.vector.memset(plane[:].bitcast(I32), 0)
 
-        raw = [stage.tile([P, PACK, H], F32, name="raw%d" % e, align_bytes=64, offset=e * RAW_BYTES) for e in range(E)]
-        w_codes = [keep.tile([P, GROUP, 2 * N], U8, name="w_codes%d" % g, align_bytes=64) for g in range(E // GROUP)]
-        wb_codes = [keep.tile([P, GROUP, PACK * N], U8, name="wb_codes%d" % g, align_bytes=64) for g in range(E // GROUP)]
+        raw, w_codes, wb_codes = {}, {}, {}
 
-        def load_wa(e):
-            nc.sync.dma_start(out=raw[e][:], in_=wa[e].rearrange("(p j) c -> p j c", j=PACK))
+        def load_wa(first, count):
+            unit = stage.tile([P, count, PACK, H], F32, name="raw%d" % first, align_bytes=64, offset=first * RAW_BYTES)
+            nc.sync.dma_start(out=unit[:], in_=wa[first : first + count].rearrange("e (p j) c -> p e j c", j=PACK))
+            for u in range(count):
+                raw[first + u] = unit[:, u]
 
-        def load_group(g):
-            es = slice(g * GROUP, (g + 1) * GROUP)
-            nc.sync.dma_start(out=w_codes[g][:].bitcast(I32), in_=w_words[es, 0].rearrange("e p b -> p e b").bitcast(I32))
-            nc.sync.dma_start(out=wb_codes[g][:].bitcast(I32), in_=wb_words[es, 0].rearrange("e p n d -> p e (n d)").bitcast(I32))
+        def load_packed(first, count):
+            es = slice(first, first + count)
+            w_tile = keep.tile([P, count, 2 * N], U8, name="w_codes%d" % first, align_bytes=64)
+            wb_tile = keep.tile([P, count, PACK * N], U8, name="wb_codes%d" % first, align_bytes=64)
+            nc.sync.dma_start(out=w_tile[:].bitcast(I32), in_=w_words[es, 0].rearrange("e p b -> p e b").bitcast(I32))
+            nc.sync.dma_start(out=wb_tile[:].bitcast(I32), in_=wb_words[es, 0].rearrange("e p n d -> p e (n d)").bitcast(I32))
+            for u in range(count):
+                w_codes[first + u] = w_tile[:, u, :]
+                wb_codes[first + u] = wb_tile[:, u, :]
 
         nc.sync.dma_start(offsets[:], offs)
         nc.sync.dma_start(out=x_table[:], in_=x_words[0].rearrange("p t d -> p (t d)").bitcast(I32))
-        load_wa(0)
         x_rows = x_scales[0].rearrange("(q r) t -> r q t", r=4)
         w_rows = w_scales[:, 0].rearrange("e (q r) n -> r q e n", r=4)
         wb_rows = wb_scales[:, 0].rearrange("e (q r) n -> r q e n", r=4)
-        for r in range(4):
-            nc.sync.dma_start(out=x_plane[r:P:32, :].bitcast(I32), in_=x_rows[r].bitcast(I32))
-        for e in range(1, E):
-            load_wa(e)
-            if e <= 4:
-                r = e - 1
+        for index, (first, count) in enumerate(LOADS):
+            load_wa(first, count)
+            if index == 0:
+                for r in range(4):
+                    nc.sync.dma_start(out=x_plane[r:P:32, :].bitcast(I32), in_=x_rows[r].bitcast(I32))
+            elif index <= 4:
+                r = index - 1
                 nc.sync.dma_start(out=w_plane[r:P:32, :, :].bitcast(I32), in_=w_rows[r].bitcast(I32))
                 nc.sync.dma_start(out=wb_plane[r:P:32, :, :].bitcast(I32), in_=wb_rows[r].bitcast(I32))
-            if e % GROUP == GROUP - 1:
-                load_group(e // GROUP)
+            if index == 4:
+                load_packed(0, EARLY)
+        load_packed(EARLY, E - EARLY)
 
         slot_words = keep.tile([P, E * C], U32, name="slot_words", align_bytes=64)
         slot_plane = keep.tile([P, E * C], U8, name="slot_plane", align_bytes=64)
@@ -81,26 +91,34 @@ def tile_moe_elr_s_none_kernel(tc, x_words, x_scales, w_words, w_scales, wa, wb_
         grouped = {}
 
         def round_wa(e):
-            grouped[e] = ring.tile([P, PACK, P, PACK], BF16, name="grouped", align_bytes=64)
-            src = raw[e][:].rearrange("p j (m t) -> p m j t", t=PACK)
-            dst = grouped[e][:].rearrange("p t m j -> p m j t")
-            cut = 0 if e < SCALAR_ALONE else LAST_VECTOR_M if e == E - 1 else VECTOR_M
-            if cut:
-                nc.vector.tensor_copy(out=dst[:, :cut], in_=src[:, :cut])
-            nc.scalar.copy(out=dst[:, cut:], in_=src[:, cut:])
+            src = raw[e].rearrange("p j (m t) -> p m j t", t=PACK)
+            dst = []
+            for half in range(2):
+                grouped[e, half] = ring.tile([P, HALF, P, PACK], BF16, name="grouped%d" % half, align_bytes=64)
+                dst.append(grouped[e, half][:].rearrange("p t m j -> p m j t"))
+            if e < SCALAR_ALONE:
+                nc.scalar.copy(out=dst[0], in_=src[:, :, :, :HALF])
+                nc.scalar.copy(out=dst[1], in_=src[:, :, :, HALF:])
+            else:
+                cut = LAST_VECTOR_M if e == E - 1 else VECTOR_M
+                nc.vector.tensor_copy(out=dst[0], in_=src[:, :, :, :HALF])
+                nc.vector.tensor_copy(out=dst[1][:, :cut], in_=src[:, :cut, :, HALF:])
+                nc.scalar.copy(out=dst[1][:, cut:], in_=src[:, cut:, :, HALF:])
 
         def quantize_wa(e):
-            wa_codes[e] = ring.tile([P, H], U32, name="wa_codes", align_bytes=64)
-            wa_plane[e] = ring.tile([P, H], U8, name="wa_plane", align_bytes=64)
-            nc.vector.quantize_mx(out=wa_codes[e][:].bitcast(FP8X4), scales=wa_plane[e][:],
-                                  in_=grouped[e][:].rearrange("p t m j -> p (t m j)"))
+            for half in range(2):
+                wa_codes[e, half] = ring.tile([P, HALF * P], U32, name="wa_codes%d" % half, align_bytes=64)
+                wa_plane[e, half] = ring.tile([P, HALF * P], U8, name="wa_plane%d" % half, align_bytes=64)
+                nc.vector.quantize_mx(out=wa_codes[e, half][:].bitcast(FP8X4), scales=wa_plane[e, half][:],
+                                      in_=grouped[e, half][:].rearrange("p t m j -> p (t m j)"))
 
         def first_product(e):
             slots = slice(e * C, (e + 1) * C)
             h_bank = psum.tile([P, PACK, C], F32, name="h_bank")
             for t in range(PACK):
-                cols = slice(t * P, (t + 1) * P)
-                nc.tensor.matmul_mx(out=h_bank[:, t, :], lhsT=wa_codes[e][:, cols].bitcast(FP8X4), lhsT_scale=wa_plane[e][:, cols],
+                half, u = divmod(t, HALF)
+                cols = slice(u * P, (u + 1) * P)
+                nc.tensor.matmul_mx(out=h_bank[:, t, :], lhsT=wa_codes[e, half][:, cols].bitcast(FP8X4), lhsT_scale=wa_plane[e, half][:, cols],
                                     rhs=slot_words[:, slots].bitcast(FP8X4), rhs_scale=slot_plane[:, slots], start=True, stop=True)
             behind = max(e + 1, SCALAR_ALONE)
             h_bf16[e] = stage.tile([P, C, PACK], BF16, name="h_bf16_%d" % e, align_bytes=64,
@@ -108,7 +126,9 @@ def tile_moe_elr_s_none_kernel(tc, x_words, x_scales, w_words, w_scales, wa, wb_
             nc.scalar.copy(out=h_bf16[e][:], in_=h_bank[:].rearrange("p t n -> p n t"))
 
         def quantize_h(e):
-            h_codes[e] = keep.tile([P, C], U32, name="h_codes%d" % e, align_bytes=64)
+            behind = max(e + 2, SCALAR_ALONE + 1)
+            h_codes[e] = stage.tile([P, C], U32, name="h_codes%d" % e, align_bytes=64,
+                                    offset=behind * RAW_BYTES + 3 * ROW_BYTES + (behind - 2 - e) * C * 4)
             h_plane[e] = keep.tile([P, C], U8, name="h_plane%d" % e, align_bytes=64)
             nc.vector.quantize_mx(out=h_codes[e][:].bitcast(FP8X4), scales=h_plane[e][:],
                                   in_=h_bf16[e][:].rearrange("p n t -> p (n t)"))
@@ -118,10 +138,9 @@ def tile_moe_elr_s_none_kernel(tc, x_words, x_scales, w_words, w_scales, wa, wb_
             for u in range(count):
                 e = first + u
                 slots = slice(e * C, (e + 1) * C)
-                g, a = divmod(e, GROUP)
-                nc.tensor.matmul_mx(out=y_bank[:, u, :], lhsT=w_codes[g][:, a, :].bitcast(FP4X4), lhsT_scale=w_plane[:, e, :],
+                nc.tensor.matmul_mx(out=y_bank[:, u, :], lhsT=w_codes[e].bitcast(FP4X4), lhsT_scale=w_plane[:, e, :],
                                     rhs=slot_words[:, slots].bitcast(FP8X4), rhs_scale=slot_plane[:, slots], start=True, stop=False)
-                nc.tensor.matmul_mx(out=y_bank[:, u, :], lhsT=wb_codes[g][:, a, :].bitcast(FP8X4), lhsT_scale=wb_plane[:, e, :],
+                nc.tensor.matmul_mx(out=y_bank[:, u, :], lhsT=wb_codes[e].bitcast(FP8X4), lhsT_scale=wb_plane[:, e, :],
                                     rhs=h_codes[e][:].bitcast(FP8X4), rhs_scale=h_plane[e][:], start=False, stop=True)
             return y_bank[:].rearrange("p u n -> p (u n)")
 
@@ -136,18 +155,21 @@ def tile_moe_elr_s_none_kernel(tc, x_words, x_scales, w_words, w_scales, wa, wb_
         for e in range(SCALAR_ALONE):
             round_wa(e)
             quantize_wa(e)
-        for i in range(SCALAR_ALONE, E + 1):
+        for i in range(SCALAR_ALONE, E + 2):
             if i < E:
                 round_wa(i)
                 quantize_wa(i)
-            for e in range(i) if i == SCALAR_ALONE else [i - 1]:
-                first_product(e)
-                quantize_h(e)
-            if i in (5, 9, 13):
-                y_banks.append(second_product(i - 5, GROUP))
+            if i <= E:
+                for e in range(i) if i == SCALAR_ALONE else [i - 1]:
+                    first_product(e)
+            if i > SCALAR_ALONE:
+                for e in range(i - 1) if i == SCALAR_ALONE + 1 else [i - 2]:
+                    quantize_h(e)
+            if i in (7, 9, 13):
+                y_banks.append(second_product(len(y_banks) * GROUP, GROUP))
             if i == 11:
                 leave(0, y_banks[:2], i, nc.scalar.copy)
-            if i == 13:
+            if i == 14:
                 leave(8, y_banks[2:], i, nc.scalar.copy)
-        leave(12, [second_product(12, 3)], 14, nc.vector.tensor_copy)
+        leave(12, [second_product(12, 3)], 15, nc.vector.tensor_copy)
         leave(15, [second_product(15, 1)], 16, nc.scalar.copy)

@@ -20,11 +20,11 @@ HALF = PACK // 2
 GROUP = 4
 GATHER = 256
 VECTOR_M = 24
-LAST_VECTOR_M = 16
+LAST_VECTOR_M = 24
 RAW_BYTES = PACK * H * 4
 ROW_BYTES = H * 4
 SCALAR_ALONE = 3
-EARLY = 12
+EARLY = 8
 LOADS = [(0, 1), (1, 1), (2, 1), (3, 1), (4, 1), (5, 1), (6, 1), (7, 1), (8, 1), (9, 1), (10, 1), (11, 1), (12, 1), (13, 1), (14, 1), (15, 1)]
 
 
@@ -74,11 +74,12 @@ def tile_moe_elr_s_none_kernel(tc, x_words, x_scales, w_words, w_scales, wa, wb_
                     nc.sync.dma_start(out=x_plane[r:P:32, :].bitcast(I32), in_=x_rows[r].bitcast(I32))
             elif index <= 4:
                 r = index - 1
-                nc.sync.dma_start(out=w_plane[r:P:32, :, :].bitcast(I32), in_=w_rows[r].bitcast(I32))
-                nc.sync.dma_start(out=wb_plane[r:P:32, :, :].bitcast(I32), in_=wb_rows[r].bitcast(I32))
-            if index == 4:
+                nc.gpsimd.dma_start(out=w_plane[r:P:32, :, :].bitcast(I32), in_=w_rows[r].bitcast(I32))
+                nc.gpsimd.dma_start(out=wb_plane[r:P:32, :, :].bitcast(I32), in_=wb_rows[r].bitcast(I32))
+            if index == 7:
                 load_packed(0, EARLY)
-        load_packed(EARLY, E - EARLY)
+        for first, count in [(8, 4), (12, 4)]:
+            load_packed(first, count)
 
         slot_words = keep.tile([P, E * C], U32, name="slot_words", align_bytes=64)
         slot_plane = keep.tile([P, E * C], U8, name="slot_plane", align_bytes=64)
@@ -144,11 +145,11 @@ def tile_moe_elr_s_none_kernel(tc, x_words, x_scales, w_words, w_scales, wa, wb_
                                     rhs=h_codes[e][:].bitcast(FP8X4), rhs_scale=h_plane[e][:], start=False, stop=True)
             return y_bank[:].rearrange("p u n -> p (u n)")
 
-        def leave(first, banks, behind, copy):
+        def leave(first, banks, behind, copies):
             widths = [bank.shape[1] for bank in banks]
             y = stage.tile([P, sum(widths)], F32, name="y%d" % first, align_bytes=64, offset=behind * RAW_BYTES + ROW_BYTES)
             for b, bank in enumerate(banks):
-                copy(out=y[:, sum(widths[:b]) : sum(widths[: b + 1])], in_=bank)
+                copies[b](out=y[:, sum(widths[:b]) : sum(widths[: b + 1])], in_=bank)
             nc.sync.dma_start(out=out[:, first * C : first * C + sum(widths)], in_=y[:])
 
         y_banks = []
@@ -165,11 +166,9 @@ def tile_moe_elr_s_none_kernel(tc, x_words, x_scales, w_words, w_scales, wa, wb_
             if i > SCALAR_ALONE:
                 for e in range(i - 1) if i == SCALAR_ALONE + 1 else [i - 2]:
                     quantize_h(e)
-            if i in (7, 9, 13):
+            if i in (9, 10):
                 y_banks.append(second_product(len(y_banks) * GROUP, GROUP))
             if i == 11:
-                leave(0, y_banks[:2], i, nc.scalar.copy)
-            if i == 14:
-                leave(8, y_banks[2:], i, nc.scalar.copy)
-        leave(12, [second_product(12, 3)], 15, nc.vector.tensor_copy)
-        leave(15, [second_product(15, 1)], 16, nc.scalar.copy)
+                leave(0, y_banks, i, [nc.scalar.copy] * 2)
+        leave(8, [second_product(8, 4)], 14, [nc.scalar.copy])
+        leave(12, [second_product(12, 3), second_product(15, 1)], 15, [nc.vector.tensor_copy, nc.scalar.copy])

@@ -17,15 +17,22 @@ FP4X4 = mybir.dt.float4_e2m1fn_x4
 P = 128
 PACK = 4
 HALF = PACK // 2
+PLANE_ROWS = 4
+QUADRANT = 32
+LIST_ROWS = 16
 GROUP = 4
 GATHER = 256
-VECTOR_M = 24
-LAST_VECTOR_M = 24
-RAW_BYTES = PACK * H * 4
-ROW_BYTES = H * 4
+
+VECTOR_M = 80
+LAST_VECTOR_M = 88
 SCALAR_ALONE = 3
-EARLY = 8
-LOADS = [(0, 1), (1, 1), (2, 1), (3, 1), (4, 1), (5, 1), (6, 1), (7, 1), (8, 1), (9, 1), (10, 1), (11, 1), (12, 1), (13, 1), (14, 1), (15, 1)]
+EARLY = 10
+
+AREA_BYTES = PACK * H * 4
+ROW_BYTES = H * 4
+Y_ROW = 1
+H_CODES_ROW = 3
+FIRST_STORE_AREA = 11
 
 
 def tile_moe_elr_s_none_kernel(tc, x_words, x_scales, w_words, w_scales, wa, wb_words, wb_scales, offs, out):
@@ -36,7 +43,7 @@ def tile_moe_elr_s_none_kernel(tc, x_words, x_scales, w_words, w_scales, wa, wb_
         stage = ctx.enter_context(tc.tile_pool(name="stage", bufs=1))
         psum = ctx.enter_context(tc.psum_pool(name="psum", bufs=4))
 
-        offsets = keep.tile([P, E * C // 16], U16, name="offsets")
+        offsets = keep.tile([P, E * C // LIST_ROWS], U16, name="offsets")
         x_table = keep.tile([P, T], I32, name="x_table", align_bytes=64)
         x_plane = keep.tile([P, T], U8, name="x_plane", align_bytes=64)
         w_plane = keep.tile([P, E, N], U8, name="w_plane", align_bytes=64)
@@ -46,72 +53,68 @@ def tile_moe_elr_s_none_kernel(tc, x_words, x_scales, w_words, w_scales, wa, wb_
 
         raw, w_codes, wb_codes = {}, {}, {}
 
-        def load_wa(first, count):
-            unit = stage.tile([P, count, PACK, H], F32, name="raw%d" % first, align_bytes=64, offset=first * RAW_BYTES)
-            nc.sync.dma_start(out=unit[:], in_=wa[first : first + count].rearrange("e (p j) c -> p e j c", j=PACK))
-            for u in range(count):
-                raw[first + u] = unit[:, u]
+        def load_wa(e):
+            raw[e] = stage.tile([P, PACK, H], F32, name="raw%d" % e, align_bytes=64, offset=e * AREA_BYTES)
+            nc.sync.dma_start(out=raw[e][:], in_=wa[e].rearrange("(p j) c -> p j c", j=PACK))
 
         def load_packed(first, count):
-            es = slice(first, first + count)
+            experts = slice(first, first + count)
             w_tile = keep.tile([P, count, 2 * N], U8, name="w_codes%d" % first, align_bytes=64)
             wb_tile = keep.tile([P, count, PACK * N], U8, name="wb_codes%d" % first, align_bytes=64)
-            nc.sync.dma_start(out=w_tile[:].bitcast(I32), in_=w_words[es, 0].rearrange("e p b -> p e b").bitcast(I32))
-            nc.sync.dma_start(out=wb_tile[:].bitcast(I32), in_=wb_words[es, 0].rearrange("e p n d -> p e (n d)").bitcast(I32))
+            nc.sync.dma_start(out=w_tile[:].bitcast(I32), in_=w_words[experts, 0].rearrange("e p b -> p e b").bitcast(I32))
+            nc.sync.dma_start(out=wb_tile[:].bitcast(I32), in_=wb_words[experts, 0].rearrange("e p n d -> p e (n d)").bitcast(I32))
             for u in range(count):
                 w_codes[first + u] = w_tile[:, u, :]
                 wb_codes[first + u] = wb_tile[:, u, :]
 
+        x_rows = x_scales[0].rearrange("(q r) t -> r q t", r=PLANE_ROWS)
+        w_rows = w_scales[:, 0].rearrange("e (q r) n -> r q e n", r=PLANE_ROWS)
+        wb_rows = wb_scales[:, 0].rearrange("e (q r) n -> r q e n", r=PLANE_ROWS)
+
         nc.sync.dma_start(offsets[:], offs)
         nc.sync.dma_start(out=x_table[:], in_=x_words[0].rearrange("p t d -> p (t d)").bitcast(I32))
-        x_rows = x_scales[0].rearrange("(q r) t -> r q t", r=4)
-        w_rows = w_scales[:, 0].rearrange("e (q r) n -> r q e n", r=4)
-        wb_rows = wb_scales[:, 0].rearrange("e (q r) n -> r q e n", r=4)
-        for index, (first, count) in enumerate(LOADS):
-            load_wa(first, count)
-            if index == 0:
-                for r in range(4):
-                    nc.sync.dma_start(out=x_plane[r:P:32, :].bitcast(I32), in_=x_rows[r].bitcast(I32))
-            elif index <= 4:
-                r = index - 1
-                nc.gpsimd.dma_start(out=w_plane[r:P:32, :, :].bitcast(I32), in_=w_rows[r].bitcast(I32))
-                nc.gpsimd.dma_start(out=wb_plane[r:P:32, :, :].bitcast(I32), in_=wb_rows[r].bitcast(I32))
-            if index == 7:
-                load_packed(0, EARLY)
-        for first, count in [(8, 4), (12, 4)]:
-            load_packed(first, count)
+        load_wa(0)
+        for r in range(PLANE_ROWS):
+            nc.sync.dma_start(out=x_plane[r:P:QUADRANT, :].bitcast(I32), in_=x_rows[r].bitcast(I32))
+        for r in range(PLANE_ROWS):
+            load_wa(1 + r)
+            nc.sync.dma_start(out=w_plane[r:P:QUADRANT, :, :].bitcast(I32), in_=w_rows[r].bitcast(I32))
+            nc.sync.dma_start(out=wb_plane[r:P:QUADRANT, :, :].bitcast(I32), in_=wb_rows[r].bitcast(I32))
+        load_packed(0, EARLY)
+        for e in range(1 + PLANE_ROWS, E):
+            load_wa(e)
+        load_packed(EARLY, E - GROUP - EARLY)
+        load_packed(E - GROUP, GROUP)
 
         slot_words = keep.tile([P, E * C], U32, name="slot_words", align_bytes=64)
         slot_plane = keep.tile([P, E * C], U8, name="slot_plane", align_bytes=64)
         for s0 in range(0, E * C, GATHER):
-            piece = offsets[:, s0 // 16 : (s0 + GATHER) // 16]
+            piece = offsets[:, s0 // LIST_ROWS : (s0 + GATHER) // LIST_ROWS]
             nc.vector.tensor_copy(slot_words[:, s0 : s0 + GATHER], x_table[:].bitcast(U32).indirect(piece))
             nc.vector.tensor_copy(slot_plane[:, s0 : s0 + GATHER], x_plane[:].indirect(piece))
 
-        wa_codes, wa_plane, h_bf16, h_codes, h_plane = {}, {}, {}, {}, {}
-        grouped = {}
+        grouped, wa_codes, wa_plane, h_bf16, h_codes, h_plane = {}, {}, {}, {}, {}, {}
 
         def round_wa(e):
-            src = raw[e].rearrange("p j (m t) -> p m j t", t=PACK)
-            dst = []
-            for half in range(2):
-                grouped[e, half] = ring.tile([P, HALF, P, PACK], BF16, name="grouped%d" % half, align_bytes=64)
-                dst.append(grouped[e, half][:].rearrange("p t m j -> p m j t"))
+            grouped[e] = ring.tile([P, PACK, P, PACK], BF16, name="grouped", align_bytes=64)
+            src = raw[e][:].rearrange("p j (m t) -> p m t j", t=PACK)
+            dst = grouped[e][:].rearrange("p t m j -> p m t j")
             if e < SCALAR_ALONE:
-                nc.scalar.copy(out=dst[0], in_=src[:, :, :, :HALF])
-                nc.scalar.copy(out=dst[1], in_=src[:, :, :, HALF:])
+                nc.scalar.copy(out=dst, in_=src)
             else:
                 cut = LAST_VECTOR_M if e == E - 1 else VECTOR_M
-                nc.vector.tensor_copy(out=dst[0], in_=src[:, :, :, :HALF])
-                nc.vector.tensor_copy(out=dst[1][:, :cut], in_=src[:, :cut, :, HALF:])
-                nc.scalar.copy(out=dst[1][:, cut:], in_=src[:, cut:, :, HALF:])
+                nc.vector.tensor_copy(out=dst[:, :cut], in_=src[:, :cut])
+                nc.scalar.copy(out=dst[:, cut:], in_=src[:, cut:])
 
         def quantize_wa(e):
-            for half in range(2):
+            for half in range(PACK // HALF):
                 wa_codes[e, half] = ring.tile([P, HALF * P], U32, name="wa_codes%d" % half, align_bytes=64)
                 wa_plane[e, half] = ring.tile([P, HALF * P], U8, name="wa_plane%d" % half, align_bytes=64)
-                nc.vector.quantize_mx(out=wa_codes[e, half][:].bitcast(FP8X4), scales=wa_plane[e, half][:],
-                                      in_=grouped[e, half][:].rearrange("p t m j -> p (t m j)"))
+                nc.vector.quantize_mx(
+                    out=wa_codes[e, half][:].bitcast(FP8X4),
+                    scales=wa_plane[e, half][:],
+                    in_=grouped[e][:, half * HALF : (half + 1) * HALF].rearrange("p t m j -> p (t m j)"),
+                )
 
         def first_product(e):
             slots = slice(e * C, (e + 1) * C)
@@ -119,43 +122,70 @@ def tile_moe_elr_s_none_kernel(tc, x_words, x_scales, w_words, w_scales, wa, wb_
             for t in range(PACK):
                 half, u = divmod(t, HALF)
                 cols = slice(u * P, (u + 1) * P)
-                nc.tensor.matmul_mx(out=h_bank[:, t, :], lhsT=wa_codes[e, half][:, cols].bitcast(FP8X4), lhsT_scale=wa_plane[e, half][:, cols],
-                                    rhs=slot_words[:, slots].bitcast(FP8X4), rhs_scale=slot_plane[:, slots], start=True, stop=True)
-            behind = max(e + 1, SCALAR_ALONE)
-            h_bf16[e] = stage.tile([P, C, PACK], BF16, name="h_bf16_%d" % e, align_bytes=64,
-                                   offset=behind * RAW_BYTES + (behind - 1 - e) * ROW_BYTES)
+                nc.tensor.matmul_mx(
+                    out=h_bank[:, t, :],
+                    lhsT=wa_codes[e, half][:, cols].bitcast(FP8X4),
+                    lhsT_scale=wa_plane[e, half][:, cols],
+                    rhs=slot_words[:, slots].bitcast(FP8X4),
+                    rhs_scale=slot_plane[:, slots],
+                    start=True,
+                    stop=True,
+                )
+            area = max(e + 1, SCALAR_ALONE)
+            h_bf16[e] = stage.tile(
+                [P, C, PACK], BF16, name="h_bf16_%d" % e, align_bytes=64, offset=area * AREA_BYTES + (area - 1 - e) * ROW_BYTES
+            )
             nc.scalar.copy(out=h_bf16[e][:], in_=h_bank[:].rearrange("p t n -> p n t"))
 
         def quantize_h(e):
-            behind = max(e + 2, SCALAR_ALONE + 1)
-            h_codes[e] = stage.tile([P, C], U32, name="h_codes%d" % e, align_bytes=64,
-                                    offset=behind * RAW_BYTES + 3 * ROW_BYTES + (behind - 2 - e) * C * 4)
+            area = max(e + 1, SCALAR_ALONE) + 1
+            h_codes[e] = stage.tile(
+                [P, C], U32, name="h_codes%d" % e, align_bytes=64,
+                offset=area * AREA_BYTES + H_CODES_ROW * ROW_BYTES + (area - 2 - e) * C * 4,
+            )
             h_plane[e] = keep.tile([P, C], U8, name="h_plane%d" % e, align_bytes=64)
-            nc.vector.quantize_mx(out=h_codes[e][:].bitcast(FP8X4), scales=h_plane[e][:],
-                                  in_=h_bf16[e][:].rearrange("p n t -> p (n t)"))
+            nc.vector.quantize_mx(
+                out=h_codes[e][:].bitcast(FP8X4), scales=h_plane[e][:], in_=h_bf16[e][:].rearrange("p n t -> p (n t)")
+            )
 
         def second_product(first, count):
             y_bank = psum.tile([P, count, C], F32, name="y_bank")
             for u in range(count):
                 e = first + u
                 slots = slice(e * C, (e + 1) * C)
-                nc.tensor.matmul_mx(out=y_bank[:, u, :], lhsT=w_codes[e].bitcast(FP4X4), lhsT_scale=w_plane[:, e, :],
-                                    rhs=slot_words[:, slots].bitcast(FP8X4), rhs_scale=slot_plane[:, slots], start=True, stop=False)
-                nc.tensor.matmul_mx(out=y_bank[:, u, :], lhsT=wb_codes[e].bitcast(FP8X4), lhsT_scale=wb_plane[:, e, :],
-                                    rhs=h_codes[e][:].bitcast(FP8X4), rhs_scale=h_plane[e][:], start=False, stop=True)
+                nc.tensor.matmul_mx(
+                    out=y_bank[:, u, :],
+                    lhsT=w_codes[e].bitcast(FP4X4),
+                    lhsT_scale=w_plane[:, e, :],
+                    rhs=slot_words[:, slots].bitcast(FP8X4),
+                    rhs_scale=slot_plane[:, slots],
+                    start=True,
+                    stop=False,
+                )
+                nc.tensor.matmul_mx(
+                    out=y_bank[:, u, :],
+                    lhsT=wb_codes[e].bitcast(FP8X4),
+                    lhsT_scale=wb_plane[:, e, :],
+                    rhs=h_codes[e][:].bitcast(FP8X4),
+                    rhs_scale=h_plane[e][:],
+                    start=False,
+                    stop=True,
+                )
             return y_bank[:].rearrange("p u n -> p (u n)")
 
-        def leave(first, banks, behind, copies):
-            widths = [bank.shape[1] for bank in banks]
-            y = stage.tile([P, sum(widths)], F32, name="y%d" % first, align_bytes=64, offset=behind * RAW_BYTES + ROW_BYTES)
+        def store(first, banks, area, copy):
+            width = banks[0].shape[1]
+            y = stage.tile(
+                [P, len(banks) * width], F32, name="y%d" % first, align_bytes=64, offset=area * AREA_BYTES + Y_ROW * ROW_BYTES
+            )
             for b, bank in enumerate(banks):
-                copies[b](out=y[:, sum(widths[:b]) : sum(widths[: b + 1])], in_=bank)
-            nc.sync.dma_start(out=out[:, first * C : first * C + sum(widths)], in_=y[:])
+                copy(out=y[:, b * width : (b + 1) * width], in_=bank)
+            nc.sync.dma_start(out=out[:, first * C : first * C + len(banks) * width], in_=y[:])
 
-        y_banks = []
         for e in range(SCALAR_ALONE):
             round_wa(e)
             quantize_wa(e)
+        early_banks = []
         for i in range(SCALAR_ALONE, E + 2):
             if i < E:
                 round_wa(i)
@@ -166,9 +196,10 @@ def tile_moe_elr_s_none_kernel(tc, x_words, x_scales, w_words, w_scales, wa, wb_
             if i > SCALAR_ALONE:
                 for e in range(i - 1) if i == SCALAR_ALONE + 1 else [i - 2]:
                     quantize_h(e)
-            if i in (9, 10):
-                y_banks.append(second_product(len(y_banks) * GROUP, GROUP))
-            if i == 11:
-                leave(0, y_banks, i, [nc.scalar.copy] * 2)
-        leave(8, [second_product(8, 4)], 14, [nc.scalar.copy])
-        leave(12, [second_product(12, 3), second_product(15, 1)], 15, [nc.vector.tensor_copy, nc.scalar.copy])
+            if i - 1 in (GROUP, 2 * GROUP):
+                early_banks.append(second_product(i - 1 - GROUP, GROUP))
+            if i == FIRST_STORE_AREA:
+                store(0, early_banks, FIRST_STORE_AREA, nc.scalar.copy)
+        store(2 * GROUP, [second_product(2 * GROUP, GROUP)], E - 2, nc.scalar.copy)
+        store(3 * GROUP, [second_product(3 * GROUP, GROUP - 1)], E - 1, nc.vector.tensor_copy)
+        store(E - 1, [second_product(E - 1, 1)], E, nc.scalar.copy)

@@ -96,15 +96,14 @@ def tile_moe_elr_s_none_kernel(tc, x_words, x_scales, w_words, w_scales, wa, wb_
         grouped, wa_codes, wa_plane, h_bf16, h_codes, h_plane = {}, {}, {}, {}, {}, {}
 
         def round_wa(e):
-            grouped[e] = ring.tile([P, PACK, P, PACK], BF16, name="grouped", align_bytes=64)
-            src = raw[e][:].rearrange("p j (m t) -> p m t j", t=PACK)
-            dst = grouped[e][:].rearrange("p t m j -> p m t j")
-            if e < SCALAR_ALONE:
-                nc.scalar.copy(out=dst, in_=src)
-            else:
-                cut = LAST_VECTOR_M if e == E - 1 else VECTOR_M
-                nc.vector.tensor_copy(out=dst[:, :cut], in_=src[:, :cut])
-                nc.scalar.copy(out=dst[:, cut:], in_=src[:, cut:])
+            cut = 0 if e < SCALAR_ALONE else LAST_VECTOR_M if e == E - 1 else VECTOR_M
+            src = raw[e][:].rearrange("p (j i) (m h u) -> p h m j u i", i=2, h=PACK // HALF, u=HALF)
+            for half in range(PACK // HALF):
+                grouped[e, half] = ring.tile([P, HALF, P, PACK], BF16, name="grouped%d" % half, align_bytes=64)
+                dst = grouped[e, half][:].rearrange("p u m (j i) -> p m j u i", i=2)
+                if cut:
+                    nc.vector.tensor_copy(out=dst[:, :cut], in_=src[:, half, :cut])
+                nc.scalar.copy(out=dst[:, cut:], in_=src[:, half, cut:])
 
         def quantize_wa(e):
             for half in range(PACK // HALF):
@@ -113,7 +112,7 @@ def tile_moe_elr_s_none_kernel(tc, x_words, x_scales, w_words, w_scales, wa, wb_
                 nc.vector.quantize_mx(
                     out=wa_codes[e, half][:].bitcast(FP8X4),
                     scales=wa_plane[e, half][:],
-                    in_=grouped[e][:, half * HALF : (half + 1) * HALF].rearrange("p t m j -> p (t m j)"),
+                    in_=grouped[e, half][:].rearrange("p u m j -> p (u m j)"),
                 )
 
         def first_product(e):

@@ -23,16 +23,15 @@ LIST_ROWS = 16
 GROUP = 4
 GATHER = 256
 
-VECTOR_M = 80
-LAST_VECTOR_M = 88
+VECTOR_SHARE = 5
 SCALAR_ALONE = 3
 EARLY = 10
 
 AREA_BYTES = PACK * H * 4
 ROW_BYTES = H * 4
 Y_ROW = 1
-H_CODES_ROW = 3
-FIRST_STORE_AREA = 11
+H_BYTES = C * PACK * 2
+FIRST_STORE_AREA = 10
 
 
 def tile_moe_elr_s_none_kernel(tc, x_words, x_scales, w_words, w_scales, wa, wb_words, wb_scales, offs, out):
@@ -54,8 +53,17 @@ def tile_moe_elr_s_none_kernel(tc, x_words, x_scales, w_words, w_scales, wa, wb_
         raw, w_codes, wb_codes = {}, {}, {}
 
         def load_wa(e):
-            raw[e] = stage.tile([P, PACK, H], F32, name="raw%d" % e, align_bytes=64, offset=e * AREA_BYTES)
-            nc.sync.dma_start(out=raw[e][:], in_=wa[e].rearrange("(p j) c -> p j c", j=PACK))
+            parts = 2 if e == E - 1 else 1
+            width = H // parts
+            raw[e] = []
+            for part in range(parts):
+                tile = stage.tile(
+                    [P, PACK, width], F32, name="raw%d_%d" % (e, part), align_bytes=64,
+                    offset=e * AREA_BYTES + (parts - 1 - part) * AREA_BYTES // parts,
+                )
+                columns = wa[e, :, part * width : (part + 1) * width]
+                nc.sync.dma_start(out=tile[:], in_=columns.rearrange("(p j) c -> p j c", j=PACK))
+                raw[e].append((part * width // PACK, tile))
 
         def load_packed(first, count):
             experts = slice(first, first + count)
@@ -79,12 +87,12 @@ def tile_moe_elr_s_none_kernel(tc, x_words, x_scales, w_words, w_scales, wa, wb_
         for r in range(PLANE_ROWS):
             load_wa(1 + r)
             nc.sync.dma_start(out=w_plane[r:P:QUADRANT, :, :].bitcast(I32), in_=w_rows[r].bitcast(I32))
-            nc.sync.dma_start(out=wb_plane[r:P:QUADRANT, :, :].bitcast(I32), in_=wb_rows[r].bitcast(I32))
+            nc.sync.dma_start(out=wb_plane[PLANE_ROWS + r : P : QUADRANT, :, :].bitcast(I32), in_=wb_rows[r].bitcast(I32))
         load_packed(0, EARLY)
         for e in range(1 + PLANE_ROWS, E):
             load_wa(e)
-        load_packed(EARLY, E - GROUP - EARLY)
-        load_packed(E - GROUP, GROUP)
+        load_packed(EARLY, GROUP)
+        load_packed(EARLY + GROUP, E - EARLY - GROUP)
 
         slot_words = keep.tile([P, E * C], U32, name="slot_words", align_bytes=64)
         slot_plane = keep.tile([P, E * C], U8, name="slot_plane", align_bytes=64)
@@ -93,17 +101,21 @@ def tile_moe_elr_s_none_kernel(tc, x_words, x_scales, w_words, w_scales, wa, wb_
             nc.vector.tensor_copy(slot_words[:, s0 : s0 + GATHER], x_table[:].bitcast(U32).indirect(piece))
             nc.vector.tensor_copy(slot_plane[:, s0 : s0 + GATHER], x_plane[:].indirect(piece))
 
+        h_banks = {}
         grouped, wa_codes, wa_plane, h_bf16, h_codes, h_plane = {}, {}, {}, {}, {}, {}
 
         def round_wa(e):
-            cut = 0 if e < SCALAR_ALONE else LAST_VECTOR_M if e == E - 1 else VECTOR_M
-            src = raw[e][:].rearrange("p (j i) (m h u) -> p h m j u i", i=2, h=PACK // HALF, u=HALF)
             for half in range(PACK // HALF):
                 grouped[e, half] = ring.tile([P, HALF, P, PACK], BF16, name="grouped%d" % half, align_bytes=64)
-                dst = grouped[e, half][:].rearrange("p u m (j i) -> p m j u i", i=2)
-                if cut:
-                    nc.vector.tensor_copy(out=dst[:, :cut], in_=src[:, half, :cut])
-                nc.scalar.copy(out=dst[:, cut:], in_=src[:, half, cut:])
+            for m0, tile in raw[e]:
+                count = tile.shape[2] // PACK
+                cut = 0 if e < SCALAR_ALONE else count // 2 if m0 == 0 and e == E - 1 else count * VECTOR_SHARE // 8
+                src = tile[:].rearrange("p (j i) (m h u) -> p h m j u i", i=2, h=PACK // HALF, u=HALF)
+                for half in range(PACK // HALF):
+                    dst = grouped[e, half][:, :, m0 : m0 + count].rearrange("p u m (j i) -> p m j u i", i=2)
+                    if cut:
+                        nc.vector.tensor_copy(out=dst[:, :cut], in_=src[:, half, :cut])
+                    nc.scalar.copy(out=dst[:, cut:], in_=src[:, half, cut:])
 
         def quantize_wa(e):
             for half in range(PACK // HALF):
@@ -117,7 +129,7 @@ def tile_moe_elr_s_none_kernel(tc, x_words, x_scales, w_words, w_scales, wa, wb_
 
         def first_product(e):
             slots = slice(e * C, (e + 1) * C)
-            h_bank = psum.tile([P, PACK, C], F32, name="h_bank")
+            h_bank = h_banks[e] = psum.tile([P, PACK, C], F32, name="h_bank")
             for t in range(PACK):
                 half, u = divmod(t, HALF)
                 cols = slice(u * P, (u + 1) * P)
@@ -130,17 +142,18 @@ def tile_moe_elr_s_none_kernel(tc, x_words, x_scales, w_words, w_scales, wa, wb_
                     start=True,
                     stop=True,
                 )
-            area = max(e + 1, SCALAR_ALONE)
+
+        def round_h(e, area):
+            h_bank = h_banks[e]
             h_bf16[e] = stage.tile(
                 [P, C, PACK], BF16, name="h_bf16_%d" % e, align_bytes=64, offset=area * AREA_BYTES + (area - 1 - e) * ROW_BYTES
             )
             nc.scalar.copy(out=h_bf16[e][:], in_=h_bank[:].rearrange("p t n -> p n t"))
 
-        def quantize_h(e):
-            area = max(e + 1, SCALAR_ALONE) + 1
+        def quantize_h(e, area):
             h_codes[e] = stage.tile(
                 [P, C], U32, name="h_codes%d" % e, align_bytes=64,
-                offset=area * AREA_BYTES + H_CODES_ROW * ROW_BYTES + (area - 2 - e) * C * 4,
+                offset=area * AREA_BYTES + H_BYTES + (area - 2 - e) * C * 4,
             )
             h_plane[e] = keep.tile([P, C], U8, name="h_plane%d" % e, align_bytes=64)
             nc.vector.quantize_mx(
@@ -164,7 +177,7 @@ def tile_moe_elr_s_none_kernel(tc, x_words, x_scales, w_words, w_scales, wa, wb_
                 nc.tensor.matmul_mx(
                     out=y_bank[:, u, :],
                     lhsT=wb_codes[e].bitcast(FP8X4),
-                    lhsT_scale=wb_plane[:, e, :],
+                    lhsT_scale=wb_plane[PLANE_ROWS:, e, :],
                     rhs=h_codes[e][:].bitcast(FP8X4),
                     rhs_scale=h_plane[e][:],
                     start=False,
@@ -173,13 +186,13 @@ def tile_moe_elr_s_none_kernel(tc, x_words, x_scales, w_words, w_scales, wa, wb_
             return y_bank[:].rearrange("p u n -> p (u n)")
 
         def store(first, banks, area, copy):
-            width = banks[0].shape[1]
-            y = stage.tile(
-                [P, len(banks) * width], F32, name="y%d" % first, align_bytes=64, offset=area * AREA_BYTES + Y_ROW * ROW_BYTES
-            )
-            for b, bank in enumerate(banks):
-                copy(out=y[:, b * width : (b + 1) * width], in_=bank)
-            nc.sync.dma_start(out=out[:, first * C : first * C + len(banks) * width], in_=y[:])
+            width = sum(bank.shape[1] for bank in banks)
+            y = stage.tile([P, width], F32, name="y%d" % first, align_bytes=64, offset=area * AREA_BYTES + Y_ROW * ROW_BYTES)
+            column = 0
+            for bank in banks:
+                copy(out=y[:, column : column + bank.shape[1]], in_=bank)
+                column += bank.shape[1]
+            nc.sync.dma_start(out=out[:, first * C : first * C + width], in_=y[:])
 
         for e in range(SCALAR_ALONE):
             round_wa(e)
@@ -192,13 +205,17 @@ def tile_moe_elr_s_none_kernel(tc, x_words, x_scales, w_words, w_scales, wa, wb_
             if i <= E:
                 for e in range(i) if i == SCALAR_ALONE else [i - 1]:
                     first_product(e)
-            if i > SCALAR_ALONE:
-                for e in range(i - 1) if i == SCALAR_ALONE + 1 else [i - 2]:
-                    quantize_h(e)
-            if i - 1 in (GROUP, 2 * GROUP):
-                early_banks.append(second_product(i - 1 - GROUP, GROUP))
-            if i == FIRST_STORE_AREA:
-                store(0, early_banks, FIRST_STORE_AREA, nc.scalar.copy)
-        store(2 * GROUP, [second_product(2 * GROUP, GROUP)], E - 2, nc.scalar.copy)
-        store(3 * GROUP, [second_product(3 * GROUP, GROUP - 1)], E - 1, nc.vector.tensor_copy)
-        store(E - 1, [second_product(E - 1, 1)], E, nc.scalar.copy)
+                if i != E - 2:
+                    for e in range(len(h_bf16), i):
+                        round_h(e, i)
+            if i > SCALAR_ALONE and i != E - 2:
+                for e in range(len(h_codes), i - 1):
+                    quantize_h(e, i)
+            if i - 1 in (GROUP, 2 * GROUP, EARLY):
+                first = len(early_banks) * GROUP
+                early_banks.append(second_product(first, i - 1 - first))
+            if i in range(FIRST_STORE_AREA, FIRST_STORE_AREA + 3):
+                group = i - FIRST_STORE_AREA
+                store(group * GROUP, [early_banks[group]], i, nc.scalar.copy)
+        store(EARLY, [second_product(EARLY, GROUP)], E - 2, nc.scalar.copy)
+        store(E - 2, [second_product(E - 2, 1), second_product(E - 1, 1)], E, nc.vector.tensor_copy)

@@ -25,13 +25,13 @@ GATHER = 256
 
 VECTOR_SHARE = 5
 SCALAR_ALONE = 3
-EARLY = 10
+EARLY = 8
 
 AREA_BYTES = PACK * H * 4
 ROW_BYTES = H * 4
 Y_ROW = 1
 H_BYTES = C * PACK * 2
-FIRST_STORE_AREA = 10
+FIRST_STORE_AREA = 12
 
 
 def tile_moe_elr_s_none_kernel(tc, x_words, x_scales, w_words, w_scales, wa, wb_words, wb_scales, offs, out):
@@ -91,8 +91,8 @@ def tile_moe_elr_s_none_kernel(tc, x_words, x_scales, w_words, w_scales, wa, wb_
         load_packed(0, EARLY)
         for e in range(1 + PLANE_ROWS, E):
             load_wa(e)
-        load_packed(EARLY, GROUP)
-        load_packed(EARLY + GROUP, E - EARLY - GROUP)
+        load_packed(EARLY, 2)
+        load_packed(EARLY + 2, E - EARLY - 2)
 
         slot_words = keep.tile([P, E * C], U32, name="slot_words", align_bytes=64)
         slot_plane = keep.tile([P, E * C], U8, name="slot_plane", align_bytes=64)
@@ -101,7 +101,7 @@ def tile_moe_elr_s_none_kernel(tc, x_words, x_scales, w_words, w_scales, wa, wb_
             nc.vector.tensor_copy(slot_words[:, s0 : s0 + GATHER], x_table[:].bitcast(U32).indirect(piece))
             nc.vector.tensor_copy(slot_plane[:, s0 : s0 + GATHER], x_plane[:].indirect(piece))
 
-        h_banks = {}
+        h_banks, shared_banks = {}, []
         grouped, wa_codes, wa_plane, h_bf16, h_codes, h_plane = {}, {}, {}, {}, {}, {}
 
         def round_wa(e):
@@ -129,12 +129,22 @@ def tile_moe_elr_s_none_kernel(tc, x_words, x_scales, w_words, w_scales, wa, wb_
 
         def first_product(e):
             slots = slice(e * C, (e + 1) * C)
-            h_bank = h_banks[e] = psum.tile([P, PACK, C], F32, name="h_bank")
+            if e < E - 1:
+                bank = psum.tile([P, PACK, C], F32, name="h_bank")
+                h_banks[e] = [bank[:]]
+                places = [bank[:, t, :] for t in range(PACK)]
+            else:
+                banks = [psum.tile([P, PACK, C], F32, name="h_bank") for half in range(PACK // HALF)]
+                for half, bank in enumerate(banks):
+                    y_pair(EARLY + half, bank[:, HALF, :])
+                    shared_banks.append(bank[:, HALF, :])
+                h_banks[e] = [bank[:, :HALF, :] for bank in banks]
+                places = [banks[t // HALF][:, t % HALF, :] for t in range(PACK)]
             for t in range(PACK):
                 half, u = divmod(t, HALF)
                 cols = slice(u * P, (u + 1) * P)
                 nc.tensor.matmul_mx(
-                    out=h_bank[:, t, :],
+                    out=places[t],
                     lhsT=wa_codes[e, half][:, cols].bitcast(FP8X4),
                     lhsT_scale=wa_plane[e, half][:, cols],
                     rhs=slot_words[:, slots].bitcast(FP8X4),
@@ -144,11 +154,14 @@ def tile_moe_elr_s_none_kernel(tc, x_words, x_scales, w_words, w_scales, wa, wb_
                 )
 
         def round_h(e, area):
-            h_bank = h_banks[e]
             h_bf16[e] = stage.tile(
                 [P, C, PACK], BF16, name="h_bf16_%d" % e, align_bytes=64, offset=area * AREA_BYTES + (area - 1 - e) * ROW_BYTES
             )
-            nc.scalar.copy(out=h_bf16[e][:], in_=h_bank[:].rearrange("p t n -> p n t"))
+            if e < E - 1:
+                nc.scalar.copy(out=h_bf16[e][:], in_=h_banks[e][0].rearrange("p t n -> p n t"))
+            else:
+                nc.vector.tensor_copy(out=h_bf16[e][:, :, :HALF], in_=h_banks[e][0].rearrange("p t n -> p n t"))
+                nc.scalar.copy(out=h_bf16[e][:, :, HALF:], in_=h_banks[e][1].rearrange("p t n -> p n t"))
 
         def quantize_h(e, area):
             h_codes[e] = stage.tile(
@@ -160,29 +173,31 @@ def tile_moe_elr_s_none_kernel(tc, x_words, x_scales, w_words, w_scales, wa, wb_
                 out=h_codes[e][:].bitcast(FP8X4), scales=h_plane[e][:], in_=h_bf16[e][:].rearrange("p n t -> p (n t)")
             )
 
+        def y_pair(e, place):
+            slots = slice(e * C, (e + 1) * C)
+            nc.tensor.matmul_mx(
+                out=place,
+                lhsT=w_codes[e].bitcast(FP4X4),
+                lhsT_scale=w_plane[:, e, :],
+                rhs=slot_words[:, slots].bitcast(FP8X4),
+                rhs_scale=slot_plane[:, slots],
+                start=True,
+                stop=False,
+            )
+            nc.tensor.matmul_mx(
+                out=place,
+                lhsT=wb_codes[e].bitcast(FP8X4),
+                lhsT_scale=wb_plane[PLANE_ROWS:, e, :],
+                rhs=h_codes[e][:].bitcast(FP8X4),
+                rhs_scale=h_plane[e][:],
+                start=False,
+                stop=True,
+            )
+
         def second_product(first, count):
             y_bank = psum.tile([P, count, C], F32, name="y_bank")
             for u in range(count):
-                e = first + u
-                slots = slice(e * C, (e + 1) * C)
-                nc.tensor.matmul_mx(
-                    out=y_bank[:, u, :],
-                    lhsT=w_codes[e].bitcast(FP4X4),
-                    lhsT_scale=w_plane[:, e, :],
-                    rhs=slot_words[:, slots].bitcast(FP8X4),
-                    rhs_scale=slot_plane[:, slots],
-                    start=True,
-                    stop=False,
-                )
-                nc.tensor.matmul_mx(
-                    out=y_bank[:, u, :],
-                    lhsT=wb_codes[e].bitcast(FP8X4),
-                    lhsT_scale=wb_plane[PLANE_ROWS:, e, :],
-                    rhs=h_codes[e][:].bitcast(FP8X4),
-                    rhs_scale=h_plane[e][:],
-                    start=False,
-                    stop=True,
-                )
+                y_pair(first + u, y_bank[:, u, :])
             return y_bank[:].rearrange("p u n -> p (u n)")
 
         def store(first, banks, area, copy):
@@ -211,11 +226,11 @@ def tile_moe_elr_s_none_kernel(tc, x_words, x_scales, w_words, w_scales, wa, wb_
             if i > SCALAR_ALONE and i != E - 2:
                 for e in range(len(h_codes), i - 1):
                     quantize_h(e, i)
-            if i - 1 in (GROUP, 2 * GROUP, EARLY):
+            if i - 1 in (GROUP, 2 * GROUP):
                 first = len(early_banks) * GROUP
                 early_banks.append(second_product(first, i - 1 - first))
-            if i in range(FIRST_STORE_AREA, FIRST_STORE_AREA + 3):
-                group = i - FIRST_STORE_AREA
-                store(group * GROUP, [early_banks[group]], i, nc.scalar.copy)
-        store(EARLY, [second_product(EARLY, GROUP)], E - 2, nc.scalar.copy)
-        store(E - 2, [second_product(E - 2, 1), second_product(E - 1, 1)], E, nc.vector.tensor_copy)
+            if i == FIRST_STORE_AREA:
+                store(0, early_banks, i, nc.scalar.copy)
+        store(EARLY, shared_banks + [second_product(EARLY + 2, 2)], E - 2, nc.scalar.copy)
+        store(E - GROUP, [second_product(E - GROUP, GROUP - 1)], E - 3, nc.scalar.copy)
+        store(E - 1, [second_product(E - 1, 1)], E, nc.vector.tensor_copy)

@@ -23,7 +23,7 @@ LIST_ROWS = 16
 GROUP = 4
 GATHER = 256
 
-VECTOR_SHARE = 5
+VECTOR_SHARE = 11
 SCALAR_ALONE = 3
 EARLY = 8
 
@@ -109,7 +109,7 @@ def tile_moe_elr_s_none_kernel(tc, x_words, x_scales, w_words, w_scales, wa, wb_
                 grouped[e, half] = ring.tile([P, HALF, P, PACK], BF16, name="grouped%d" % half, align_bytes=64)
             for m0, tile in raw[e]:
                 count = tile.shape[2] // PACK
-                cut = 0 if e < SCALAR_ALONE else count // 2 if m0 == 0 and e == E - 1 else count * VECTOR_SHARE // 8
+                cut = 0 if e < SCALAR_ALONE else count * VECTOR_SHARE // 16 if e < E - 1 else count // 2 if m0 == 0 else count * 5 // 8
                 src = tile[:].rearrange("p (j i) (m h u) -> p h m j u i", i=2, h=PACK // HALF, u=HALF)
                 for half in range(PACK // HALF):
                     dst = grouped[e, half][:, :, m0 : m0 + count].rearrange("p u m (j i) -> p m j u i", i=2)
@@ -229,8 +229,8 @@ def tile_moe_elr_s_none_kernel(tc, x_words, x_scales, w_words, w_scales, wa, wb_
             if i - 1 in (GROUP, 2 * GROUP):
                 first = len(early_banks) * GROUP
                 early_banks.append(second_product(first, i - 1 - first))
-            if i == FIRST_STORE_AREA:
-                store(0, early_banks, i, nc.scalar.copy)
+            if i - 2 in (GROUP, 2 * GROUP):
+                store(i - 2 - GROUP, [early_banks[-1]], i, nc.scalar.copy)
         store(EARLY, shared_banks + [second_product(EARLY + 2, 2)], E - 2, nc.scalar.copy)
         store(E - GROUP, [second_product(E - GROUP, GROUP - 1)], E - 3, nc.scalar.copy)
         store(E - 1, [second_product(E - 1, 1)], E, nc.vector.tensor_copy)

@@ -46,8 +46,8 @@ def tile_moe_elr_s_none_kernel(tc, x_words, x_scales, w_words, w_scales, wa, wb_
         x_table = keep.tile([P, T], I32, name="x_table", align_bytes=64)
         x_plane = keep.tile([P, T], U8, name="x_plane", align_bytes=64)
         w_plane = keep.tile([P, E, N], U8, name="w_plane", align_bytes=64)
-        wb_plane = keep.tile([P, E, N], U8, name="wb_plane", align_bytes=64)
-        for plane in (x_plane, w_plane, wb_plane):
+        wb_plane = w_plane
+        for plane in (x_plane, w_plane):
             nc.vector.memset(plane[:].bitcast(I32), 0)
 
         raw, w_codes, wb_codes = {}, {}, {}
@@ -86,11 +86,12 @@ def tile_moe_elr_s_none_kernel(tc, x_words, x_scales, w_words, w_scales, wa, wb_
             nc.sync.dma_start(out=x_plane[r:P:QUADRANT, :].bitcast(I32), in_=x_rows[r].bitcast(I32))
         for r in range(PLANE_ROWS):
             load_wa(1 + r)
-            nc.sync.dma_start(out=w_plane[r:P:QUADRANT, :, :].bitcast(I32), in_=w_rows[r].bitcast(I32))
-            nc.sync.dma_start(out=wb_plane[PLANE_ROWS + r : P : QUADRANT, :, :].bitcast(I32), in_=wb_rows[r].bitcast(I32))
-        load_packed(0, EARLY)
+            nc.gpsimd.dma_start(out=w_plane[r:P:QUADRANT, :, :].bitcast(I32), in_=w_rows[r].bitcast(I32))
+            nc.gpsimd.dma_start(out=wb_plane[PLANE_ROWS + r : P : QUADRANT, :, :].bitcast(I32), in_=wb_rows[r].bitcast(I32))
         for e in range(1 + PLANE_ROWS, E):
             load_wa(e)
+            if e == EARLY:
+                load_packed(0, EARLY)
         load_packed(EARLY, 2)
         load_packed(EARLY + 2, E - EARLY - 2)
 
@@ -229,8 +230,8 @@ def tile_moe_elr_s_none_kernel(tc, x_words, x_scales, w_words, w_scales, wa, wb_
             if i - 1 in (GROUP, 2 * GROUP):
                 first = len(early_banks) * GROUP
                 early_banks.append(second_product(first, i - 1 - first))
-            if i - 2 in (GROUP, 2 * GROUP):
-                store(i - 2 - GROUP, [early_banks[-1]], i, nc.scalar.copy)
+            if i - 2 - EARLY in (0, 1):
+                store((i - 2 - EARLY) * GROUP, [early_banks[i - 2 - EARLY]], i, nc.scalar.copy)
         store(EARLY, shared_banks + [second_product(EARLY + 2, 2)], E - 2, nc.scalar.copy)
         store(E - GROUP, [second_product(E - GROUP, GROUP - 1)], E - 3, nc.scalar.copy)
         store(E - 1, [second_product(E - 1, 1)], E, nc.vector.tensor_copy)

@@ -23,9 +23,10 @@ LIST_ROWS = 16
 GROUP = 4
 GATHER = 256
 
-VECTOR_SHARE = 11
+VECTOR_SHARE = 21
 SCALAR_ALONE = 3
 EARLY = 8
+PAIRED = (3, 5, 7)
 
 AREA_BYTES = PACK * H * 4
 ROW_BYTES = H * 4
@@ -53,27 +54,22 @@ def tile_moe_elr_s_none_kernel(tc, x_words, x_scales, w_words, w_scales, wa, wb_
         raw, w_codes, wb_codes = {}, {}, {}
 
         def load_wa(e):
-            parts = 2 if e == E - 1 else 1
-            width = H // parts
-            raw[e] = []
-            for part in range(parts):
-                tile = stage.tile(
-                    [P, PACK, width], F32, name="raw%d_%d" % (e, part), align_bytes=64,
-                    offset=e * AREA_BYTES + (parts - 1 - part) * AREA_BYTES // parts,
-                )
-                columns = wa[e, :, part * width : (part + 1) * width]
-                nc.sync.dma_start(out=tile[:], in_=columns.rearrange("(p j) c -> p j c", j=PACK))
-                raw[e].append((part * width // PACK, tile))
-
-        def load_packed(first, count):
-            experts = slice(first, first + count)
-            w_tile = keep.tile([P, count, 2 * N], U8, name="w_codes%d" % first, align_bytes=64)
-            wb_tile = keep.tile([P, count, PACK * N], U8, name="wb_codes%d" % first, align_bytes=64)
-            nc.sync.dma_start(out=w_tile[:].bitcast(I32), in_=w_words[experts, 0].rearrange("e p b -> p e b").bitcast(I32))
-            nc.sync.dma_start(out=wb_tile[:].bitcast(I32), in_=wb_words[experts, 0].rearrange("e p n d -> p e (n d)").bitcast(I32))
+            if e in raw:
+                return
+            count = 2 if e in PAIRED else 1
+            tile = stage.tile([P, count, PACK * H], F32, name="raw%d" % e, align_bytes=64, offset=e * AREA_BYTES)
+            nc.sync.dma_start(out=tile[:], in_=wa[e : e + count].rearrange("e (p j) c -> p e (j c)", j=PACK))
             for u in range(count):
-                w_codes[first + u] = w_tile[:, u, :]
-                wb_codes[first + u] = wb_tile[:, u, :]
+                raw[e + u] = [(0, tile[:, u, :])]
+
+        def load_packed(codes, words, name, first, count):
+            tile = keep.tile([P, count, words.shape[2]], U8, name="%s%d" % (name, first), align_bytes=64)
+            nc.sync.dma_start(out=tile[:].bitcast(I32), in_=words[:, first : first + count].bitcast(I32))
+            for u in range(count):
+                codes[first + u] = tile[:, u, :]
+
+        w_source = w_words[:, 0].rearrange("e p b -> p e b")
+        wb_source = wb_words[:, 0].rearrange("e p n d -> p e (n d)")
 
         x_rows = x_scales[0].rearrange("(q r) t -> r q t", r=PLANE_ROWS)
         w_rows = w_scales[:, 0].rearrange("e (q r) n -> r q e n", r=PLANE_ROWS)
@@ -86,14 +82,16 @@ def tile_moe_elr_s_none_kernel(tc, x_words, x_scales, w_words, w_scales, wa, wb_
             nc.sync.dma_start(out=x_plane[r:P:QUADRANT, :].bitcast(I32), in_=x_rows[r].bitcast(I32))
         for r in range(PLANE_ROWS):
             load_wa(1 + r)
-            nc.gpsimd.dma_start(out=w_plane[r:P:QUADRANT, :, :].bitcast(I32), in_=w_rows[r].bitcast(I32))
-            nc.gpsimd.dma_start(out=wb_plane[PLANE_ROWS + r : P : QUADRANT, :, :].bitcast(I32), in_=wb_rows[r].bitcast(I32))
+            nc.sync.dma_start(out=w_plane[r:P:QUADRANT, :, :].bitcast(I32), in_=w_rows[r].bitcast(I32))
+            nc.sync.dma_start(out=wb_plane[PLANE_ROWS + r : P : QUADRANT, :, :].bitcast(I32), in_=wb_rows[r].bitcast(I32))
+        load_packed(w_codes, w_source, "w_codes", 0, EARLY)
+        load_packed(wb_codes, wb_source, "wb_codes", 0, EARLY)
         for e in range(1 + PLANE_ROWS, E):
             load_wa(e)
-            if e == EARLY:
-                load_packed(0, EARLY)
-        load_packed(EARLY, 2)
-        load_packed(EARLY + 2, E - EARLY - 2)
+        load_packed(w_codes, w_source, "w_codes", EARLY, 2)
+        load_packed(wb_codes, wb_source, "wb_codes", EARLY, 2)
+        load_packed(w_codes, w_source, "w_codes", EARLY + 2, E - EARLY - 2)
+        load_packed(wb_codes, wb_source, "wb_codes", EARLY + 2, E - EARLY - 2)
 
         slot_words = keep.tile([P, E * C], U32, name="slot_words", align_bytes=64)
         slot_plane = keep.tile([P, E * C], U8, name="slot_plane", align_bytes=64)
@@ -109,9 +107,9 @@ def tile_moe_elr_s_none_kernel(tc, x_words, x_scales, w_words, w_scales, wa, wb_
             for half in range(PACK // HALF):
                 grouped[e, half] = ring.tile([P, HALF, P, PACK], BF16, name="grouped%d" % half, align_bytes=64)
             for m0, tile in raw[e]:
-                count = tile.shape[2] // PACK
-                cut = 0 if e < SCALAR_ALONE else count * VECTOR_SHARE // 16 if e < E - 1 else count // 2 if m0 == 0 else count * 5 // 8
-                src = tile[:].rearrange("p (j i) (m h u) -> p h m j u i", i=2, h=PACK // HALF, u=HALF)
+                count = P
+                cut = 0 if e < SCALAR_ALONE else count * VECTOR_SHARE // 32
+                src = tile.rearrange("p (j i m h u) -> p h m j u i", j=2, i=2, h=PACK // HALF, u=HALF)
                 for half in range(PACK // HALF):
                     dst = grouped[e, half][:, :, m0 : m0 + count].rearrange("p u m (j i) -> p m j u i", i=2)
                     if cut:
@@ -131,11 +129,11 @@ def tile_moe_elr_s_none_kernel(tc, x_words, x_scales, w_words, w_scales, wa, wb_
         def first_product(e):
             slots = slice(e * C, (e + 1) * C)
             if e < E - 1:
-                bank = psum.tile([P, PACK, C], F32, name="h_bank")
+                bank = psum.tile([P, PACK, C], F32, name="h_bank", bufs=2)
                 h_banks[e] = [bank[:]]
                 places = [bank[:, t, :] for t in range(PACK)]
             else:
-                banks = [psum.tile([P, PACK, C], F32, name="h_bank") for half in range(PACK // HALF)]
+                banks = [psum.tile([P, PACK, C], F32, name="last_bank", bufs=2) for half in range(PACK // HALF)]
                 for half, bank in enumerate(banks):
                     y_pair(EARLY + half, bank[:, HALF, :])
                     shared_banks.append(bank[:, HALF, :])
@@ -195,8 +193,8 @@ def tile_moe_elr_s_none_kernel(tc, x_words, x_scales, w_words, w_scales, wa, wb_
                 stop=True,
             )
 
-        def second_product(first, count):
-            y_bank = psum.tile([P, count, C], F32, name="y_bank")
+        def second_product(first, count, tag="y_bank", bufs=4):
+            y_bank = psum.tile([P, count, C], F32, name=tag, bufs=bufs)
             for u in range(count):
                 y_pair(first + u, y_bank[:, u, :])
             return y_bank[:].rearrange("p u n -> p (u n)")
@@ -221,17 +219,17 @@ def tile_moe_elr_s_none_kernel(tc, x_words, x_scales, w_words, w_scales, wa, wb_
             if i <= E:
                 for e in range(i) if i == SCALAR_ALONE else [i - 1]:
                     first_product(e)
-                if i != E - 2:
-                    for e in range(len(h_bf16), i):
-                        round_h(e, i)
-            if i > SCALAR_ALONE and i != E - 2:
+                for e in range(len(h_bf16), i):
+                    round_h(e, i)
+            if i > SCALAR_ALONE:
                 for e in range(len(h_codes), i - 1):
                     quantize_h(e, i)
-            if i - 1 in (GROUP, 2 * GROUP):
-                first = len(early_banks) * GROUP
-                early_banks.append(second_product(first, i - 1 - first))
-            if i - 2 - EARLY in (0, 1):
-                store((i - 2 - EARLY) * GROUP, [early_banks[i - 2 - EARLY]], i, nc.scalar.copy)
+            if i - 1 == GROUP:
+                early_banks.append(second_product(0, GROUP))
+            if i - 2 == GROUP:
+                store(0, early_banks, i, nc.scalar.copy)
+            if i == E - 1:
+                store(GROUP, [second_product(GROUP, GROUP, "h_bank", 2)], i, nc.scalar.copy)
         store(EARLY, shared_banks + [second_product(EARLY + 2, 2)], E - 2, nc.scalar.copy)
         store(E - GROUP, [second_product(E - GROUP, GROUP - 1)], E - 3, nc.scalar.copy)
         store(E - 1, [second_product(E - 1, 1)], E, nc.vector.tensor_copy)

@@ -20,19 +20,23 @@ HALF = PACK // 2
 PLANE_ROWS = 4
 QUADRANT = 32
 LIST_ROWS = 16
-GROUP = 4
 GATHER = 256
+GROUP = 4
+BANK_BYTES = 2048
+H_BANKS = 4
+LAST = E - 1
 
-VECTOR_SHARE = 21
+WA_LOADS = (1, 1, 1, 3, 3, 2, 1, 1, 1, 1, 1)
+VECTOR_M = 76
+LAST_VECTOR_M = (84, 64)
 SCALAR_ALONE = 3
-EARLY = 8
-PAIRED = (3, 5, 7)
+SPLIT_FROM = 14
+W_EARLY = 4
+WB_EARLY = 0
 
 AREA_BYTES = PACK * H * 4
-ROW_BYTES = H * 4
-Y_ROW = 1
 H_BYTES = C * PACK * 2
-FIRST_STORE_AREA = 12
+Y_OFFSET = 2 * H_BYTES
 
 
 def tile_moe_elr_s_none_kernel(tc, x_words, x_scales, w_words, w_scales, wa, wb_words, wb_scales, offs, out):
@@ -41,26 +45,28 @@ def tile_moe_elr_s_none_kernel(tc, x_words, x_scales, w_words, w_scales, wa, wb_
         keep = ctx.enter_context(tc.tile_pool(name="keep", bufs=1))
         ring = ctx.enter_context(tc.tile_pool(name="ring", bufs=6))
         stage = ctx.enter_context(tc.tile_pool(name="stage", bufs=1))
-        psum = ctx.enter_context(tc.psum_pool(name="psum", bufs=4))
+        psum = ctx.enter_context(tc.psum_pool(name="psum", bufs=1))
 
         offsets = keep.tile([P, E * C // LIST_ROWS], U16, name="offsets")
         x_table = keep.tile([P, T], I32, name="x_table", align_bytes=64)
         x_plane = keep.tile([P, T], U8, name="x_plane", align_bytes=64)
-        w_plane = keep.tile([P, E, N], U8, name="w_plane", align_bytes=64)
-        wb_plane = w_plane
-        for plane in (x_plane, w_plane):
+        planes = keep.tile([P, E, N], U8, name="planes", align_bytes=64)
+        for plane in (x_plane, planes):
             nc.vector.memset(plane[:].bitcast(I32), 0)
 
+        starts = [sum(WA_LOADS[:g]) for g in range(len(WA_LOADS))]
         raw, w_codes, wb_codes = {}, {}, {}
 
-        def load_wa(e):
-            if e in raw:
-                return
-            count = 2 if e in PAIRED else 1
-            tile = stage.tile([P, count, PACK * H], F32, name="raw%d" % e, align_bytes=64, offset=e * AREA_BYTES)
-            nc.sync.dma_start(out=tile[:], in_=wa[e : e + count].rearrange("e (p j) c -> p e (j c)", j=PACK))
+        def load_wa(g):
+            first, count = starts[g], WA_LOADS[g]
+            tile = stage.tile([P, count, PACK * H], F32, name="raw%d" % first, align_bytes=64, offset=first * AREA_BYTES)
+            nc.sync.dma_start(out=tile[:], in_=wa[first : first + count].rearrange("e (p j) c -> p e (j c)", j=PACK))
             for u in range(count):
-                raw[e + u] = [(0, tile[:, u, :])]
+                raw[first + u] = tile[:, u, :]
+
+        def load_rows(plane, start, rows):
+            for r in range(PLANE_ROWS):
+                nc.sync.dma_start(out=plane[start + r : P : QUADRANT].bitcast(I32), in_=rows[r].bitcast(I32))
 
         def load_packed(codes, words, name, first, count):
             tile = keep.tile([P, count, words.shape[2]], U8, name="%s%d" % (name, first), align_bytes=64)
@@ -70,7 +76,6 @@ def tile_moe_elr_s_none_kernel(tc, x_words, x_scales, w_words, w_scales, wa, wb_
 
         w_source = w_words[:, 0].rearrange("e p b -> p e b")
         wb_source = wb_words[:, 0].rearrange("e p n d -> p e (n d)")
-
         x_rows = x_scales[0].rearrange("(q r) t -> r q t", r=PLANE_ROWS)
         w_rows = w_scales[:, 0].rearrange("e (q r) n -> r q e n", r=PLANE_ROWS)
         wb_rows = wb_scales[:, 0].rearrange("e (q r) n -> r q e n", r=PLANE_ROWS)
@@ -78,158 +83,161 @@ def tile_moe_elr_s_none_kernel(tc, x_words, x_scales, w_words, w_scales, wa, wb_
         nc.sync.dma_start(offsets[:], offs)
         nc.sync.dma_start(out=x_table[:], in_=x_words[0].rearrange("p t d -> p (t d)").bitcast(I32))
         load_wa(0)
-        for r in range(PLANE_ROWS):
-            nc.sync.dma_start(out=x_plane[r:P:QUADRANT, :].bitcast(I32), in_=x_rows[r].bitcast(I32))
-        for r in range(PLANE_ROWS):
-            load_wa(1 + r)
-            nc.sync.dma_start(out=w_plane[r:P:QUADRANT, :, :].bitcast(I32), in_=w_rows[r].bitcast(I32))
-            nc.sync.dma_start(out=wb_plane[PLANE_ROWS + r : P : QUADRANT, :, :].bitcast(I32), in_=wb_rows[r].bitcast(I32))
-        load_packed(w_codes, w_source, "w_codes", 0, EARLY)
-        load_packed(wb_codes, wb_source, "wb_codes", 0, EARLY)
-        for e in range(1 + PLANE_ROWS, E):
-            load_wa(e)
-        load_packed(w_codes, w_source, "w_codes", EARLY, 2)
-        load_packed(wb_codes, wb_source, "wb_codes", EARLY, 2)
-        load_packed(w_codes, w_source, "w_codes", EARLY + 2, E - EARLY - 2)
-        load_packed(wb_codes, wb_source, "wb_codes", EARLY + 2, E - EARLY - 2)
+        load_rows(x_plane[:], 0, x_rows)
+        for g in range(1, 4):
+            load_wa(g)
+        load_rows(planes[:], 0, w_rows)
+        load_wa(4)
+        load_rows(planes[:], PLANE_ROWS, wb_rows)
+        load_wa(5)
+        for g in range(6, len(WA_LOADS) - 1):
+            load_wa(g)
+        load_packed(w_codes, w_source, "w_codes", 0, E)
+        load_wa(len(WA_LOADS) - 1)
+        for first in range(WB_EARLY, E, GROUP):
+            load_packed(wb_codes, wb_source, "wb_codes", first, GROUP)
 
         slot_words = keep.tile([P, E * C], U32, name="slot_words", align_bytes=64)
         slot_plane = keep.tile([P, E * C], U8, name="slot_plane", align_bytes=64)
         for s0 in range(0, E * C, GATHER):
-            piece = offsets[:, s0 // LIST_ROWS : (s0 + GATHER) // LIST_ROWS]
-            nc.vector.tensor_copy(slot_words[:, s0 : s0 + GATHER], x_table[:].bitcast(U32).indirect(piece))
-            nc.vector.tensor_copy(slot_plane[:, s0 : s0 + GATHER], x_plane[:].indirect(piece))
+            s1 = min(s0 + GATHER, E * C)
+            piece = offsets[:, s0 // LIST_ROWS : s1 // LIST_ROWS]
+            nc.vector.tensor_copy(slot_words[:, s0:s1], x_table[:].bitcast(U32).indirect(piece))
+            nc.vector.tensor_copy(slot_plane[:, s0:s1], x_plane[:].indirect(piece))
 
-        h_banks, shared_banks = {}, []
-        grouped, wa_codes, wa_plane, h_bf16, h_codes, h_plane = {}, {}, {}, {}, {}, {}
+        wa_codes, wa_plane, h_banks, h_bf16, h_codes, h_plane, y_place = {}, {}, {}, {}, {}, {}, {}
 
-        def round_wa(e):
-            for half in range(PACK // HALF):
-                grouped[e, half] = ring.tile([P, HALF, P, PACK], BF16, name="grouped%d" % half, align_bytes=64)
-            for m0, tile in raw[e]:
-                count = P
-                cut = 0 if e < SCALAR_ALONE else count * VECTOR_SHARE // 32
-                src = tile.rearrange("p (j i m h u) -> p h m j u i", j=2, i=2, h=PACK // HALF, u=HALF)
-                for half in range(PACK // HALF):
-                    dst = grouped[e, half][:, :, m0 : m0 + count].rearrange("p u m (j i) -> p m j u i", i=2)
-                    if cut:
-                        nc.vector.tensor_copy(out=dst[:, :cut], in_=src[:, half, :cut])
-                    nc.scalar.copy(out=dst[:, cut:], in_=src[:, half, cut:])
+        def bank(name, index, count=PACK):
+            tile = psum.tile([P, count, C], F32, name=name, offset=index * BANK_BYTES)
+            return tile[:]
 
-        def quantize_wa(e):
-            for half in range(PACK // HALF):
-                wa_codes[e, half] = ring.tile([P, HALF * P], U32, name="wa_codes%d" % half, align_bytes=64)
-                wa_plane[e, half] = ring.tile([P, HALF * P], U8, name="wa_plane%d" % half, align_bytes=64)
-                nc.vector.quantize_mx(
-                    out=wa_codes[e, half][:].bitcast(FP8X4),
-                    scales=wa_plane[e, half][:],
-                    in_=grouped[e, half][:].rearrange("p u m j -> p (u m j)"),
+        def share(dst, src, cut):
+            if cut:
+                nc.vector.tensor_copy(out=dst[:, :cut], in_=src[:, :cut])
+            nc.scalar.copy(out=dst[:, cut:], in_=src[:, cut:])
+
+        def quantize_wa(e, t0, grouped, name):
+            count = grouped.shape[1]
+            codes = ring.tile([P, count * P], U32, name="wa_codes" + name, align_bytes=64, bufs=1 if name else 5)
+            plane = ring.tile([P, count * P], U8, name="wa_plane" + name, align_bytes=64, bufs=1 if name else 5)
+            nc.vector.quantize_mx(out=codes[:].bitcast(FP8X4), scales=plane[:], in_=grouped.rearrange("p u m j -> p (u m j)"))
+            for u in range(count):
+                wa_codes[e, t0 + u] = codes[:, u * P : (u + 1) * P]
+                wa_plane[e, t0 + u] = plane[:, u * P : (u + 1) * P]
+
+        def prepare_wa(e):
+            cut = 0 if e < SCALAR_ALONE else VECTOR_M
+            if e < SPLIT_FROM:
+                grouped = ring.tile([P, PACK, P, PACK], BF16, name="grouped", align_bytes=64, bufs=5)
+                share(
+                    grouped[:].rearrange("p t m (j i) -> p m j t i", i=2),
+                    raw[e].rearrange("p (j i m t) -> p m j t i", j=2, i=2, t=PACK),
+                    cut,
                 )
+                quantize_wa(e, 0, grouped[:], "")
+                return
+            halves = [ring.tile([P, HALF, P, PACK], BF16, name="grouped%d" % half, align_bytes=64, bufs=2) for half in range(2)]
+            src = raw[e].rearrange("p (j i m h u) -> p h m j u i", j=2, i=2, h=2, u=HALF)
+            for half, tile in enumerate(halves):
+                share(tile[:].rearrange("p u m (j i) -> p m j u i", i=2), src[:, half], LAST_VECTOR_M[half] if e == LAST else cut)
+            for half, tile in enumerate(halves):
+                if e < LAST:
+                    quantize_wa(e, HALF * half, tile[:], "h%d" % half)
+                else:
+                    for u in range(HALF):
+                        quantize_wa(e, HALF * half + u, tile[:, u : u + 1], "q%d" % (HALF * half + u))
 
         def first_product(e):
             slots = slice(e * C, (e + 1) * C)
-            if e < E - 1:
-                bank = psum.tile([P, PACK, C], F32, name="h_bank", bufs=2)
-                h_banks[e] = [bank[:]]
-                places = [bank[:, t, :] for t in range(PACK)]
+            if e < LAST:
+                h_banks[e] = [bank("h%d" % e, e % H_BANKS)]
             else:
-                banks = [psum.tile([P, PACK, C], F32, name="last_bank", bufs=2) for half in range(PACK // HALF)]
-                for half, bank in enumerate(banks):
-                    y_pair(EARLY + half, bank[:, HALF, :])
-                    shared_banks.append(bank[:, HALF, :])
-                h_banks[e] = [bank[:, :HALF, :] for bank in banks]
-                places = [banks[t // HALF][:, t % HALF, :] for t in range(PACK)]
+                h_banks[e] = [bank("h_last0", e % H_BANKS, HALF), bank("h_last1", 1, HALF)]
+            places = [place[:, u, :] for place in h_banks[e] for u in range(place.shape[1])]
             for t in range(PACK):
-                half, u = divmod(t, HALF)
-                cols = slice(u * P, (u + 1) * P)
                 nc.tensor.matmul_mx(
                     out=places[t],
-                    lhsT=wa_codes[e, half][:, cols].bitcast(FP8X4),
-                    lhsT_scale=wa_plane[e, half][:, cols],
+                    lhsT=wa_codes[e, t].bitcast(FP8X4),
+                    lhsT_scale=wa_plane[e, t],
                     rhs=slot_words[:, slots].bitcast(FP8X4),
                     rhs_scale=slot_plane[:, slots],
                     start=True,
                     stop=True,
                 )
 
-        def round_h(e, area):
-            h_bf16[e] = stage.tile(
-                [P, C, PACK], BF16, name="h_bf16_%d" % e, align_bytes=64, offset=area * AREA_BYTES + (area - 1 - e) * ROW_BYTES
-            )
-            if e < E - 1:
+        def held(shape, dtype, name, offset):
+            if offset is None:
+                return keep.tile(shape, dtype, name=name, align_bytes=64)
+            return stage.tile(shape, dtype, name=name, align_bytes=64, offset=offset)
+
+        def round_h(e):
+            h_bf16[e] = held([P, C, PACK], BF16, "h_bf16_%d" % e, (e + 1) * AREA_BYTES if e + 1 in starts[:-1] else None)
+            if e < LAST:
                 nc.scalar.copy(out=h_bf16[e][:], in_=h_banks[e][0].rearrange("p t n -> p n t"))
             else:
                 nc.vector.tensor_copy(out=h_bf16[e][:, :, :HALF], in_=h_banks[e][0].rearrange("p t n -> p n t"))
-                nc.scalar.copy(out=h_bf16[e][:, :, HALF:], in_=h_banks[e][1].rearrange("p t n -> p n t"))
+                nc.vector.tensor_copy(out=h_bf16[e][:, :, HALF:], in_=h_banks[e][1].rearrange("p t n -> p n t"))
 
-        def quantize_h(e, area):
-            h_codes[e] = stage.tile(
-                [P, C], U32, name="h_codes%d" % e, align_bytes=64,
-                offset=area * AREA_BYTES + H_BYTES + (area - 2 - e) * C * 4,
-            )
+        def quantize_h(e):
+            h_codes[e] = held([P, C], U32, "h_codes%d" % e, (e + 2) * AREA_BYTES + H_BYTES if e + 2 in starts[:-1] else None)
             h_plane[e] = keep.tile([P, C], U8, name="h_plane%d" % e, align_bytes=64)
             nc.vector.quantize_mx(
                 out=h_codes[e][:].bitcast(FP8X4), scales=h_plane[e][:], in_=h_bf16[e][:].rearrange("p n t -> p (n t)")
             )
 
-        def y_pair(e, place):
-            slots = slice(e * C, (e + 1) * C)
-            nc.tensor.matmul_mx(
-                out=place,
-                lhsT=w_codes[e].bitcast(FP4X4),
-                lhsT_scale=w_plane[:, e, :],
-                rhs=slot_words[:, slots].bitcast(FP8X4),
-                rhs_scale=slot_plane[:, slots],
-                start=True,
-                stop=False,
-            )
-            nc.tensor.matmul_mx(
-                out=place,
-                lhsT=wb_codes[e].bitcast(FP8X4),
-                lhsT_scale=wb_plane[PLANE_ROWS:, e, :],
-                rhs=h_codes[e][:].bitcast(FP8X4),
-                rhs_scale=h_plane[e][:],
-                start=False,
-                stop=True,
-            )
+        def open_y(first, count, index):
+            y_place[first] = bank("y%d" % first, index, count)
 
-        def second_product(first, count, tag="y_bank", bufs=4):
-            y_bank = psum.tile([P, count, C], F32, name=tag, bufs=bufs)
+        def frozen_products(first, opens, closes):
+            place = y_place[first]
+            count = place.shape[1]
             for u in range(count):
-                y_pair(first + u, y_bank[:, u, :])
-            return y_bank[:].rearrange("p u n -> p (u n)")
+                slots = slice((first + u) * C, (first + u + 1) * C)
+                nc.tensor.matmul_mx(
+                    out=place[:, u, :],
+                    lhsT=w_codes[first + u].bitcast(FP4X4),
+                    lhsT_scale=planes[:, first + u, :],
+                    rhs=slot_words[:, slots].bitcast(FP8X4),
+                    rhs_scale=slot_plane[:, slots],
+                    start=opens and u == 0,
+                    stop=closes and u == count - 1,
+                )
 
-        def store(first, banks, area, copy):
-            width = sum(bank.shape[1] for bank in banks)
-            y = stage.tile([P, width], F32, name="y%d" % first, align_bytes=64, offset=area * AREA_BYTES + Y_ROW * ROW_BYTES)
-            column = 0
-            for bank in banks:
-                copy(out=y[:, column : column + bank.shape[1]], in_=bank)
-                column += bank.shape[1]
-            nc.sync.dma_start(out=out[:, first * C : first * C + width], in_=y[:])
+        def second_products(first, opens, closes):
+            place = y_place[first]
+            count = place.shape[1]
+            for u in range(count):
+                e = first + u
+                nc.tensor.matmul_mx(
+                    out=place[:, u, :],
+                    lhsT=wb_codes[e].bitcast(FP8X4),
+                    lhsT_scale=planes[PLANE_ROWS:, e, :],
+                    rhs=h_codes[e][:].bitcast(FP8X4),
+                    rhs_scale=h_plane[e][:],
+                    start=opens and u == 0,
+                    stop=closes and u == count - 1,
+                )
 
-        for e in range(SCALAR_ALONE):
-            round_wa(e)
-            quantize_wa(e)
-        early_banks = []
-        for i in range(SCALAR_ALONE, E + 2):
+        def store(firsts, copies, offset=None):
+            width = sum(y_place[first].shape[1] for first in firsts)
+            y = held([P, width, C], F32, "y_out%d" % firsts[0], offset)
+            for first, copy in zip(firsts, copies):
+                place = y_place[first]
+                copy(out=y[:, first - firsts[0] : first - firsts[0] + place.shape[1]], in_=place)
+            nc.sync.dma_start(out=out[:, firsts[0] * C : (firsts[0] + width) * C], in_=y[:].rearrange("p u n -> p (u n)"))
+
+        for i in range(E + 2):
             if i < E:
-                round_wa(i)
-                quantize_wa(i)
-            if i <= E:
-                for e in range(i) if i == SCALAR_ALONE else [i - 1]:
-                    first_product(e)
-                for e in range(len(h_bf16), i):
-                    round_h(e, i)
-            if i > SCALAR_ALONE:
-                for e in range(len(h_codes), i - 1):
-                    quantize_h(e, i)
-            if i - 1 == GROUP:
-                early_banks.append(second_product(0, GROUP))
-            if i - 2 == GROUP:
-                store(0, early_banks, i, nc.scalar.copy)
-            if i == E - 1:
-                store(GROUP, [second_product(GROUP, GROUP, "h_bank", 2)], i, nc.scalar.copy)
-        store(EARLY, shared_banks + [second_product(EARLY + 2, 2)], E - 2, nc.scalar.copy)
-        store(E - GROUP, [second_product(E - GROUP, GROUP - 1)], E - 3, nc.scalar.copy)
-        store(E - 1, [second_product(E - 1, 1)], E, nc.vector.tensor_copy)
+                prepare_wa(i)
+            if 0 <= i - 1 <= LAST:
+                first_product(i - 1)
+                round_h(i - 1)
+            if 0 <= i - 2:
+                quantize_h(i - 2)
+            if i - 1 == LAST - 1:
+                for first, count, index in ((0, 4, 4), (4, 4, 5), (8, 4, 6), (12, 3, 0), (15, 1, 7)):
+                    open_y(first, count, index)
+                    frozen_products(first, True, False)
+        for first in (0, 4, 8, 12, 15):
+            second_products(first, False, True)
+            store([first], [nc.vector.tensor_copy if first > 8 else nc.scalar.copy])

@@ -26,11 +26,11 @@ BANK_BYTES = 2048
 H_BANKS = 4
 LAST = E - 1
 
-WA_LOADS = (1, 1, 1, 3, 3, 2, 1, 1, 1, 1, 1)
-VECTOR_M = 76
+WA_LOADS = (1, 1, 1, 2, 2, 2, 1, 1, 1, 1, 1, 1, 1)
+VECTOR_M = 84
 LAST_VECTOR_M = (84, 64)
 SCALAR_ALONE = 3
-SPLIT_FROM = 14
+SPLIT_FROM = 0
 W_EARLY = 4
 WB_EARLY = 0
 
@@ -64,8 +64,8 @@ def tile_moe_elr_s_none_kernel(tc, x_words, x_scales, w_words, w_scales, wa, wb_
             for u in range(count):
                 raw[first + u] = tile[:, u, :]
 
-        def load_rows(plane, start, rows):
-            for r in range(PLANE_ROWS):
+        def load_rows(plane, start, rows, which):
+            for r in which:
                 nc.sync.dma_start(out=plane[start + r : P : QUADRANT].bitcast(I32), in_=rows[r].bitcast(I32))
 
         def load_packed(codes, words, name, first, count):
@@ -83,14 +83,12 @@ def tile_moe_elr_s_none_kernel(tc, x_words, x_scales, w_words, w_scales, wa, wb_
         nc.sync.dma_start(offsets[:], offs)
         nc.sync.dma_start(out=x_table[:], in_=x_words[0].rearrange("p t d -> p (t d)").bitcast(I32))
         load_wa(0)
-        load_rows(x_plane[:], 0, x_rows)
-        for g in range(1, 4):
-            load_wa(g)
-        load_rows(planes[:], 0, w_rows)
-        load_wa(4)
-        load_rows(planes[:], PLANE_ROWS, wb_rows)
-        load_wa(5)
-        for g in range(6, len(WA_LOADS) - 1):
+        load_rows(x_plane[:], 0, x_rows, range(PLANE_ROWS))
+        for r in range(PLANE_ROWS):
+            load_wa(1 + r)
+            load_rows(planes[:], 0, w_rows, [r])
+            load_rows(planes[:], PLANE_ROWS, wb_rows, [r])
+        for g in range(1 + PLANE_ROWS, len(WA_LOADS) - 1):
             load_wa(g)
         load_packed(w_codes, w_source, "w_codes", 0, E)
         load_wa(len(WA_LOADS) - 1)
@@ -118,8 +116,8 @@ def tile_moe_elr_s_none_kernel(tc, x_words, x_scales, w_words, w_scales, wa, wb_
 
         def quantize_wa(e, t0, grouped, name):
             count = grouped.shape[1]
-            codes = ring.tile([P, count * P], U32, name="wa_codes" + name, align_bytes=64, bufs=1 if name else 5)
-            plane = ring.tile([P, count * P], U8, name="wa_plane" + name, align_bytes=64, bufs=1 if name else 5)
+            codes = ring.tile([P, count * P], U32, name="wa_codes" + name, align_bytes=64, bufs=1 if "q" in name else 5)
+            plane = ring.tile([P, count * P], U8, name="wa_plane" + name, align_bytes=64, bufs=1 if "q" in name else 5)
             nc.vector.quantize_mx(out=codes[:].bitcast(FP8X4), scales=plane[:], in_=grouped.rearrange("p u m j -> p (u m j)"))
             for u in range(count):
                 wa_codes[e, t0 + u] = codes[:, u * P : (u + 1) * P]
@@ -136,7 +134,7 @@ def tile_moe_elr_s_none_kernel(tc, x_words, x_scales, w_words, w_scales, wa, wb_
                 )
                 quantize_wa(e, 0, grouped[:], "")
                 return
-            halves = [ring.tile([P, HALF, P, PACK], BF16, name="grouped%d" % half, align_bytes=64, bufs=2) for half in range(2)]
+            halves = [ring.tile([P, HALF, P, PACK], BF16, name="grouped%d" % half, align_bytes=64, bufs=5) for half in range(2)]
             src = raw[e].rearrange("p (j i m h u) -> p h m j u i", j=2, i=2, h=2, u=HALF)
             for half, tile in enumerate(halves):
                 share(tile[:].rearrange("p u m (j i) -> p m j u i", i=2), src[:, half], LAST_VECTOR_M[half] if e == LAST else cut)

@@ -20,16 +20,16 @@ HALF = PACK // 2
 PLANE_ROWS = 4
 QUADRANT = 32
 LIST_ROWS = 16
-GATHER = 256
+GATHER = 384
 GROUP = 4
 BANK_BYTES = 2048
 H_BANKS = 4
 LAST = E - 1
 
-WA_LOADS = (1, 1, 1, 2, 2, 2, 1, 1, 1, 1, 1, 1, 1)
-VECTOR_M = 84
+WA_LOADS = (2, 3, 3, 2, 2, 1, 1, 1, 1)
+VECTOR_M = 76
 LAST_VECTOR_M = (84, 64)
-SCALAR_ALONE = 3
+SCALAR_ALONE = 2
 SPLIT_FROM = 0
 W_EARLY = 4
 WB_EARLY = 0
@@ -84,11 +84,13 @@ def tile_moe_elr_s_none_kernel(tc, x_words, x_scales, w_words, w_scales, wa, wb_
         nc.sync.dma_start(out=x_table[:], in_=x_words[0].rearrange("p t d -> p (t d)").bitcast(I32))
         load_wa(0)
         load_rows(x_plane[:], 0, x_rows, range(PLANE_ROWS))
+        for g in range(1, 3):
+            load_wa(g)
         for r in range(PLANE_ROWS):
-            load_wa(1 + r)
             load_rows(planes[:], 0, w_rows, [r])
             load_rows(planes[:], PLANE_ROWS, wb_rows, [r])
-        for g in range(1 + PLANE_ROWS, len(WA_LOADS) - 1):
+            load_wa(3 + r)
+        for g in range(3 + PLANE_ROWS, len(WA_LOADS) - 1):
             load_wa(g)
         load_packed(w_codes, w_source, "w_codes", 0, E)
         load_wa(len(WA_LOADS) - 1)

@@ -26,8 +26,8 @@ BANK_BYTES = 2048
 H_BANKS = 4
 LAST = E - 1
 
-WA_LOADS = (2, 3, 3, 2, 2, 1, 1, 1, 1)
-VECTOR_M = 76
+WA_LOADS = (2, 3, 2, 2, 2, 1, 1, 1, 1, 1)
+VECTOR_M = 80
 LAST_VECTOR_M = (84, 64)
 SCALAR_ALONE = 2
 SPLIT_FROM = 0
@@ -84,13 +84,13 @@ def tile_moe_elr_s_none_kernel(tc, x_words, x_scales, w_words, w_scales, wa, wb_
         nc.sync.dma_start(out=x_table[:], in_=x_words[0].rearrange("p t d -> p (t d)").bitcast(I32))
         load_wa(0)
         load_rows(x_plane[:], 0, x_rows, range(PLANE_ROWS))
-        for g in range(1, 3):
+        for g in range(1, 2):
             load_wa(g)
         for r in range(PLANE_ROWS):
             load_rows(planes[:], 0, w_rows, [r])
             load_rows(planes[:], PLANE_ROWS, wb_rows, [r])
-            load_wa(3 + r)
-        for g in range(3 + PLANE_ROWS, len(WA_LOADS) - 1):
+            load_wa(2 + r)
+        for g in range(2 + PLANE_ROWS, len(WA_LOADS) - 1):
             load_wa(g)
         load_packed(w_codes, w_source, "w_codes", 0, E)
         load_wa(len(WA_LOADS) - 1)
@@ -235,9 +235,15 @@ def tile_moe_elr_s_none_kernel(tc, x_words, x_scales, w_words, w_scales, wa, wb_
             if 0 <= i - 2:
                 quantize_h(i - 2)
             if i - 1 == LAST - 1:
-                for first, count, index in ((0, 4, 4), (4, 4, 5), (8, 4, 6), (12, 3, 0), (15, 1, 7)):
+                for first, count, index in ((0, 2, 4), (2, 2, 5), (4, 4, 6), (8, 4, 7), (12, 3, 0), (15, 1, 2)):
                     open_y(first, count, index)
                     frozen_products(first, True, False)
-        for first in (0, 4, 8, 12, 15):
-            second_products(first, False, True)
-            store([first], [nc.vector.tensor_copy if first > 8 else nc.scalar.copy])
+        for firsts, copies in (
+            ([0, 2], [nc.scalar.copy, nc.scalar.copy]),
+            ([4], [nc.scalar.copy]),
+            ([8], [nc.scalar.copy]),
+            ([12, 15], [nc.vector.tensor_copy, nc.vector.tensor_copy]),
+        ):
+            for first in firsts:
+                second_products(first, False, True)
+            store(firsts, copies)

@@ -28,7 +28,7 @@ LAST = E - 1
 
 WA_LOADS = (2, 3, 2, 2, 2, 1, 1, 1, 1, 1)
 VECTOR_M = 80
-LAST_VECTOR_M = (84, 64)
+LAST_VECTOR_M = (84, 72)
 SCALAR_ALONE = 2
 SPLIT_FROM = 0
 W_EARLY = 4
@@ -84,13 +84,13 @@ def tile_moe_elr_s_none_kernel(tc, x_words, x_scales, w_words, w_scales, wa, wb_
         nc.sync.dma_start(out=x_table[:], in_=x_words[0].rearrange("p t d -> p (t d)").bitcast(I32))
         load_wa(0)
         load_rows(x_plane[:], 0, x_rows, range(PLANE_ROWS))
-        for g in range(1, 2):
+        for g in range(1, 4):
             load_wa(g)
         for r in range(PLANE_ROWS):
             load_rows(planes[:], 0, w_rows, [r])
             load_rows(planes[:], PLANE_ROWS, wb_rows, [r])
-            load_wa(2 + r)
-        for g in range(2 + PLANE_ROWS, len(WA_LOADS) - 1):
+            load_wa(4 + r)
+        for g in range(4 + PLANE_ROWS, len(WA_LOADS) - 1):
             load_wa(g)
         load_packed(w_codes, w_source, "w_codes", 0, E)
         load_wa(len(WA_LOADS) - 1)
@@ -179,7 +179,7 @@ def tile_moe_elr_s_none_kernel(tc, x_words, x_scales, w_words, w_scales, wa, wb_
                 nc.vector.tensor_copy(out=h_bf16[e][:, :, HALF:], in_=h_banks[e][1].rearrange("p t n -> p n t"))
 
         def quantize_h(e):
-            h_codes[e] = held([P, C], U32, "h_codes%d" % e, (e + 2) * AREA_BYTES + H_BYTES if e + 2 in starts[:-1] else None)
+            h_codes[e] = held([P, C], U32, "h_codes%d" % e, min(e + 2, LAST) * AREA_BYTES + H_BYTES if e + 2 in starts[:-1] or e == LAST - 1 else None)
             h_plane[e] = keep.tile([P, C], U8, name="h_plane%d" % e, align_bytes=64)
             nc.vector.quantize_mx(
                 out=h_codes[e][:].bitcast(FP8X4), scales=h_plane[e][:], in_=h_bf16[e][:].rearrange("p n t -> p (n t)")

@@ -48,9 +48,9 @@ def tile_moe_elr_s_none_kernel(tc, x_words, x_scales, w_words, w_scales, wa, wb_
         psum = ctx.enter_context(tc.psum_pool(name="psum", bufs=1))
 
         offsets = keep.tile([P, E * C // LIST_ROWS], U16, name="offsets")
-        x_table = keep.tile([P, T], I32, name="x_table", align_bytes=64)
-        x_plane = keep.tile([P, T], U8, name="x_plane", align_bytes=64)
-        planes = keep.tile([P, E, N], U8, name="planes", align_bytes=64)
+        x_table = keep.tile([P, T], I32, name="x_table", align_bytes=256)
+        x_plane = keep.tile([P, T], U8, name="x_plane", align_bytes=256)
+        planes = keep.tile([P, E, N], U8, name="planes", align_bytes=256)
         for plane in (x_plane, planes):
             nc.vector.memset(plane[:].bitcast(I32), 0)
 
@@ -59,7 +59,7 @@ def tile_moe_elr_s_none_kernel(tc, x_words, x_scales, w_words, w_scales, wa, wb_
 
         def load_wa(g):
             first, count = starts[g], WA_LOADS[g]
-            tile = stage.tile([P, count, PACK * H], F32, name="raw%d" % first, align_bytes=64, offset=first * AREA_BYTES)
+            tile = stage.tile([P, count, PACK * H], F32, name="raw%d" % first, align_bytes=256, offset=first * AREA_BYTES)
             nc.sync.dma_start(out=tile[:], in_=wa[first : first + count].rearrange("e (p j) c -> p e (j c)", j=PACK))
             for u in range(count):
                 raw[first + u] = tile[:, u, :]
@@ -69,7 +69,7 @@ def tile_moe_elr_s_none_kernel(tc, x_words, x_scales, w_words, w_scales, wa, wb_
                 nc.sync.dma_start(out=plane[start + r : P : QUADRANT].bitcast(I32), in_=rows[r].bitcast(I32))
 
         def load_packed(codes, words, name, first, count):
-            tile = keep.tile([P, count, words.shape[2]], U8, name="%s%d" % (name, first), align_bytes=64)
+            tile = keep.tile([P, count, words.shape[2]], U8, name="%s%d" % (name, first), align_bytes=256)
             nc.sync.dma_start(out=tile[:].bitcast(I32), in_=words[:, first : first + count].bitcast(I32))
             for u in range(count):
                 codes[first + u] = tile[:, u, :]
@@ -97,8 +97,8 @@ def tile_moe_elr_s_none_kernel(tc, x_words, x_scales, w_words, w_scales, wa, wb_
         for first in range(WB_EARLY, E, GROUP):
             load_packed(wb_codes, wb_source, "wb_codes", first, GROUP)
 
-        slot_words = keep.tile([P, E * C], U32, name="slot_words", align_bytes=64)
-        slot_plane = keep.tile([P, E * C], U8, name="slot_plane", align_bytes=64)
+        slot_words = keep.tile([P, E * C], U32, name="slot_words", align_bytes=256)
+        slot_plane = keep.tile([P, E * C], U8, name="slot_plane", align_bytes=256)
         for s0 in range(0, E * C, GATHER):
             s1 = min(s0 + GATHER, E * C)
             piece = offsets[:, s0 // LIST_ROWS : s1 // LIST_ROWS]
@@ -118,8 +118,8 @@ def tile_moe_elr_s_none_kernel(tc, x_words, x_scales, w_words, w_scales, wa, wb_
 
         def quantize_wa(e, t0, grouped, name):
             count = grouped.shape[1]
-            codes = ring.tile([P, count * P], U32, name="wa_codes" + name, align_bytes=64, bufs=1 if "q" in name else 5)
-            plane = ring.tile([P, count * P], U8, name="wa_plane" + name, align_bytes=64, bufs=1 if "q" in name else 5)
+            codes = ring.tile([P, count * P], U32, name="wa_codes" + name, align_bytes=256, bufs=1 if "q" in name else 5)
+            plane = ring.tile([P, count * P], U8, name="wa_plane" + name, align_bytes=256, bufs=1 if "q" in name else 5)
             nc.vector.quantize_mx(out=codes[:].bitcast(FP8X4), scales=plane[:], in_=grouped.rearrange("p u m j -> p (u m j)"))
             for u in range(count):
                 wa_codes[e, t0 + u] = codes[:, u * P : (u + 1) * P]
@@ -128,7 +128,7 @@ def tile_moe_elr_s_none_kernel(tc, x_words, x_scales, w_words, w_scales, wa, wb_
         def prepare_wa(e):
             cut = 0 if e < SCALAR_ALONE else VECTOR_M
             if e < SPLIT_FROM:
-                grouped = ring.tile([P, PACK, P, PACK], BF16, name="grouped", align_bytes=64, bufs=5)
+                grouped = ring.tile([P, PACK, P, PACK], BF16, name="grouped", align_bytes=256, bufs=5)
                 share(
                     grouped[:].rearrange("p t m (j i) -> p m j t i", i=2),
                     raw[e].rearrange("p (j i m t) -> p m j t i", j=2, i=2, t=PACK),
@@ -136,7 +136,7 @@ def tile_moe_elr_s_none_kernel(tc, x_words, x_scales, w_words, w_scales, wa, wb_
                 )
                 quantize_wa(e, 0, grouped[:], "")
                 return
-            halves = [ring.tile([P, HALF, P, PACK], BF16, name="grouped%d" % half, align_bytes=64, bufs=5) for half in range(2)]
+            halves = [ring.tile([P, HALF, P, PACK], BF16, name="grouped%d" % half, align_bytes=256, bufs=5) for half in range(2)]
             src = raw[e].rearrange("p (j i m h u) -> p h m j u i", j=2, i=2, h=2, u=HALF)
             for half, tile in enumerate(halves):
                 share(tile[:].rearrange("p u m (j i) -> p m j u i", i=2), src[:, half], LAST_VECTOR_M[half] if e == LAST else cut)
@@ -167,8 +167,8 @@ def tile_moe_elr_s_none_kernel(tc, x_words, x_scales, w_words, w_scales, wa, wb_
 
         def held(shape, dtype, name, offset):
             if offset is None:
-                return keep.tile(shape, dtype, name=name, align_bytes=64)
-            return stage.tile(shape, dtype, name=name, align_bytes=64, offset=offset)
+                return keep.tile(shape, dtype, name=name, align_bytes=256)
+            return stage.tile(shape, dtype, name=name, align_bytes=256, offset=offset)
 
         def round_h(e):
             h_bf16[e] = held([P, C, PACK], BF16, "h_bf16_%d" % e, (e + 1) * AREA_BYTES if e + 1 in starts[:-1] else None)
@@ -180,7 +180,7 @@ def tile_moe_elr_s_none_kernel(tc, x_words, x_scales, w_words, w_scales, wa, wb_
 
         def quantize_h(e):
             h_codes[e] = held([P, C], U32, "h_codes%d" % e, min(e + 2, LAST) * AREA_BYTES + H_BYTES if e + 2 in starts[:-1] or e == LAST - 1 else None)
-            h_plane[e] = keep.tile([P, C], U8, name="h_plane%d" % e, align_bytes=64)
+            h_plane[e] = keep.tile([P, C], U8, name="h_plane%d" % e, align_bytes=256)
             nc.vector.quantize_mx(
                 out=h_codes[e][:].bitcast(FP8X4), scales=h_plane[e][:], in_=h_bf16[e][:].rearrange("p n t -> p (n t)")
             )

@@ -30,9 +30,8 @@ WA_LOADS = (2, 3, 2, 2, 2, 1, 1, 1, 1, 1)
 VECTOR_M = 80
 LAST_VECTOR_M = (84, 72)
 SCALAR_ALONE = 2
-SPLIT_FROM = 0
-W_EARLY = 4
-WB_EARLY = 0
+ROWS_FROM = 2
+ROW_PITCH = 256
 
 AREA_BYTES = PACK * H * 4
 H_BYTES = C * PACK * 2
@@ -50,9 +49,10 @@ def tile_moe_elr_s_none_kernel(tc, x_words, x_scales, w_words, w_scales, wa, wb_
         offsets = keep.tile([P, E * C // LIST_ROWS], U16, name="offsets")
         x_table = keep.tile([P, T], I32, name="x_table", align_bytes=256)
         x_plane = keep.tile([P, T], U8, name="x_plane", align_bytes=256)
-        planes = keep.tile([P, E, N], U8, name="planes", align_bytes=256)
-        for plane in (x_plane, planes):
-            nc.vector.memset(plane[:].bitcast(I32), 0)
+        pitched = keep.tile([P, E, ROW_PITCH], U8, name="planes", align_bytes=256)
+        planes = pitched[:, :, :N]
+        for plane in (x_plane[:], planes):
+            nc.vector.memset(plane.bitcast(I32), 0)
 
         starts = [sum(WA_LOADS[:g]) for g in range(len(WA_LOADS))]
         raw, w_codes, wb_codes = {}, {}, {}
@@ -84,17 +84,17 @@ def tile_moe_elr_s_none_kernel(tc, x_words, x_scales, w_words, w_scales, wa, wb_
         nc.sync.dma_start(out=x_table[:], in_=x_words[0].rearrange("p t d -> p (t d)").bitcast(I32))
         load_wa(0)
         load_rows(x_plane[:], 0, x_rows, range(PLANE_ROWS))
-        for g in range(1, 4):
+        for g in range(1, ROWS_FROM):
             load_wa(g)
         for r in range(PLANE_ROWS):
-            load_rows(planes[:], 0, w_rows, [r])
-            load_rows(planes[:], PLANE_ROWS, wb_rows, [r])
-            load_wa(4 + r)
-        for g in range(4 + PLANE_ROWS, len(WA_LOADS) - 1):
+            load_rows(planes, 0, w_rows, [r])
+            load_rows(planes, PLANE_ROWS, wb_rows, [r])
+            load_wa(ROWS_FROM + r)
+        for g in range(ROWS_FROM + PLANE_ROWS, len(WA_LOADS) - 1):
             load_wa(g)
         load_packed(w_codes, w_source, "w_codes", 0, E)
         load_wa(len(WA_LOADS) - 1)
-        for first in range(WB_EARLY, E, GROUP):
+        for first in range(0, E, GROUP):
             load_packed(wb_codes, wb_source, "wb_codes", first, GROUP)
 
         slot_words = keep.tile([P, E * C], U32, name="slot_words", align_bytes=256)
@@ -127,15 +127,6 @@ def tile_moe_elr_s_none_kernel(tc, x_words, x_scales, w_words, w_scales, wa, wb_
 
         def prepare_wa(e):
             cut = 0 if e < SCALAR_ALONE else VECTOR_M
-            if e < SPLIT_FROM:
-                grouped = ring.tile([P, PACK, P, PACK], BF16, name="grouped", align_bytes=256, bufs=5)
-                share(
-                    grouped[:].rearrange("p t m (j i) -> p m j t i", i=2),
-                    raw[e].rearrange("p (j i m t) -> p m j t i", j=2, i=2, t=PACK),
-                    cut,
-                )
-                quantize_wa(e, 0, grouped[:], "")
-                return
             halves = [ring.tile([P, HALF, P, PACK], BF16, name="grouped%d" % half, align_bytes=256, bufs=5) for half in range(2)]
             src = raw[e].rearrange("p (j i m h u) -> p h m j u i", j=2, i=2, h=2, u=HALF)
             for half, tile in enumerate(halves):

@@ -46,7 +46,7 @@ def tile_moe_elr_s_none_kernel(tc, x_words, x_scales, w_words, w_scales, wa, wb_
         stage = ctx.enter_context(tc.tile_pool(name="stage", bufs=1))
         psum = ctx.enter_context(tc.psum_pool(name="psum", bufs=1))
 
-        offsets = keep.tile([P, E * C // LIST_ROWS], U16, name="offsets")
+        offsets = keep.tile([P, E * C // LIST_ROWS], U16, name="offsets", align_bytes=256)
         x_table = keep.tile([P, T], I32, name="x_table", align_bytes=256)
         x_plane = keep.tile([P, T], U8, name="x_plane", align_bytes=256)
         pitched = keep.tile([P, E, ROW_PITCH], U8, name="planes", align_bytes=256)
@@ -80,8 +80,8 @@ def tile_moe_elr_s_none_kernel(tc, x_words, x_scales, w_words, w_scales, wa, wb_
         w_rows = w_scales[:, 0].rearrange("e (q r) n -> r q e n", r=PLANE_ROWS)
         wb_rows = wb_scales[:, 0].rearrange("e (q r) n -> r q e n", r=PLANE_ROWS)
 
-        nc.sync.dma_start(offsets[:], offs)
         nc.sync.dma_start(out=x_table[:], in_=x_words[0].rearrange("p t d -> p (t d)").bitcast(I32))
+        nc.sync.dma_start(offsets[:], offs)
         load_wa(0)
         load_rows(x_plane[:], 0, x_rows, range(PLANE_ROWS))
         for g in range(1, ROWS_FROM):
@@ -140,14 +140,10 @@ def tile_moe_elr_s_none_kernel(tc, x_words, x_scales, w_words, w_scales, wa, wb_
 
         def first_product(e):
             slots = slice(e * C, (e + 1) * C)
-            if e < LAST:
-                h_banks[e] = [bank("h%d" % e, e % H_BANKS)]
-            else:
-                h_banks[e] = [bank("h_last0", e % H_BANKS, HALF), bank("h_last1", 1, HALF)]
-            places = [place[:, u, :] for place in h_banks[e] for u in range(place.shape[1])]
+            h_banks[e] = bank("h%d" % e, e % H_BANKS)
             for t in range(PACK):
                 nc.tensor.matmul_mx(
-                    out=places[t],
+                    out=h_banks[e][:, t, :],
                     lhsT=wa_codes[e, t].bitcast(FP8X4),
                     lhsT_scale=wa_plane[e, t],
                     rhs=slot_words[:, slots].bitcast(FP8X4),
@@ -163,11 +159,8 @@ def tile_moe_elr_s_none_kernel(tc, x_words, x_scales, w_words, w_scales, wa, wb_
 
         def round_h(e):
             h_bf16[e] = held([P, C, PACK], BF16, "h_bf16_%d" % e, (e + 1) * AREA_BYTES if e + 1 in starts[:-1] else None)
-            if e < LAST:
-                nc.scalar.copy(out=h_bf16[e][:], in_=h_banks[e][0].rearrange("p t n -> p n t"))
-            else:
-                nc.vector.tensor_copy(out=h_bf16[e][:, :, :HALF], in_=h_banks[e][0].rearrange("p t n -> p n t"))
-                nc.vector.tensor_copy(out=h_bf16[e][:, :, HALF:], in_=h_banks[e][1].rearrange("p t n -> p n t"))
+            copy = nc.scalar.copy if e < LAST else nc.vector.tensor_copy
+            copy(out=h_bf16[e][:], in_=h_banks[e].rearrange("p t n -> p n t"))
 
         def quantize_h(e):
             h_codes[e] = held([P, C], U32, "h_codes%d" % e, min(e + 2, LAST) * AREA_BYTES + H_BYTES if e + 2 in starts[:-1] or e == LAST - 1 else None)

@@ -30,6 +30,7 @@ WA_LOADS = (2, 3, 2, 2, 2, 1, 1, 1, 1, 1)
 VECTOR_M = 80
 LAST_VECTOR_M = (84, 72)
 SCALAR_ALONE = 2
+BEFORE_LAST = 2
 ROWS_FROM = 2
 ROW_PITCH = 256
 
@@ -210,24 +211,32 @@ def tile_moe_elr_s_none_kernel(tc, x_words, x_scales, w_words, w_scales, wa, wb_
                 copy(out=y[:, first - firsts[0] : first - firsts[0] + place.shape[1]], in_=place)
             nc.sync.dma_start(out=out[:, firsts[0] * C : (firsts[0] + width) * C], in_=y[:].rearrange("p u n -> p (u n)"))
 
+        stores = (
+            ([0], [nc.scalar.copy]),
+            ([4, 6], [nc.scalar.copy, nc.scalar.copy]),
+            ([8, 10], [nc.scalar.copy, nc.scalar.copy]),
+            ([12, 15], [nc.vector.tensor_copy, nc.vector.tensor_copy]),
+        )
+
+        def finish(firsts, copies):
+            for first in firsts:
+                second_products(first, False, True)
+            store(firsts, copies)
+
         for i in range(E + 2):
             if i < E:
                 prepare_wa(i)
+            if i - 1 == LAST:
+                for group in stores[:BEFORE_LAST]:
+                    finish(*group)
             if 0 <= i - 1 <= LAST:
                 first_product(i - 1)
                 round_h(i - 1)
             if 0 <= i - 2:
                 quantize_h(i - 2)
             if i - 1 == LAST - 1:
-                for first, count, index in ((0, 2, 4), (2, 2, 5), (4, 4, 6), (8, 4, 7), (12, 3, 0), (15, 1, 2)):
+                for first, count, index in ((0, 4, 4), (4, 2, 5), (6, 2, 6), (8, 2, 7), (12, 3, 0), (10, 2, 1), (15, 1, 2)):
                     open_y(first, count, index)
                     frozen_products(first, True, False)
-        for firsts, copies in (
-            ([0, 2], [nc.scalar.copy, nc.scalar.copy]),
-            ([4], [nc.scalar.copy]),
-            ([8], [nc.scalar.copy]),
-            ([12, 15], [nc.vector.tensor_copy, nc.vector.tensor_copy]),
-        ):
-            for first in firsts:
-                second_products(first, False, True)
-            store(firsts, copies)
+        for group in stores[BEFORE_LAST:]:
+            finish(*group)

@@ -48,8 +48,8 @@ def tile_moe_elr_s_none_kernel(tc, x_words, x_scales, w_words, w_scales, wa, wb_
         psum = ctx.enter_context(tc.psum_pool(name="psum", bufs=1))
 
         offsets = keep.tile([P, E * C // LIST_ROWS], U16, name="offsets", align_bytes=256)
-        x_table = keep.tile([P, T], I32, name="x_table", align_bytes=256)
-        x_plane = keep.tile([P, T], U8, name="x_plane", align_bytes=256)
+        x_table = keep.tile([P, T], I32, name="x_table", align_bytes=512)
+        x_plane = keep.tile([P, T], U8, name="x_plane", align_bytes=512)
         pitched = keep.tile([P, E, ROW_PITCH], U8, name="planes", align_bytes=256)
         planes = pitched[:, :, :N]
         for plane in (x_plane[:], planes):
@@ -60,7 +60,7 @@ def tile_moe_elr_s_none_kernel(tc, x_words, x_scales, w_words, w_scales, wa, wb_
 
         def load_wa(g):
             first, count = starts[g], WA_LOADS[g]
-            tile = stage.tile([P, count, PACK * H], F32, name="raw%d" % first, align_bytes=256, offset=first * AREA_BYTES)
+            tile = stage.tile([P, count, PACK * H], F32, name="raw%d" % first, align_bytes=512, offset=first * AREA_BYTES)
             nc.sync.dma_start(out=tile[:], in_=wa[first : first + count].rearrange("e (p j) c -> p e (j c)", j=PACK))
             for u in range(count):
                 raw[first + u] = tile[:, u, :]
@@ -70,7 +70,7 @@ def tile_moe_elr_s_none_kernel(tc, x_words, x_scales, w_words, w_scales, wa, wb_
                 nc.sync.dma_start(out=plane[start + r : P : QUADRANT].bitcast(I32), in_=rows[r].bitcast(I32))
 
         def load_packed(codes, words, name, first, count):
-            tile = keep.tile([P, count, words.shape[2]], U8, name="%s%d" % (name, first), align_bytes=256)
+            tile = keep.tile([P, count, words.shape[2]], U8, name="%s%d" % (name, first), align_bytes=512)
             nc.sync.dma_start(out=tile[:].bitcast(I32), in_=words[:, first : first + count].bitcast(I32))
             for u in range(count):
                 codes[first + u] = tile[:, u, :]
@@ -155,7 +155,7 @@ def tile_moe_elr_s_none_kernel(tc, x_words, x_scales, w_words, w_scales, wa, wb_
 
         def held(shape, dtype, name, offset):
             if offset is None:
-                return keep.tile(shape, dtype, name=name, align_bytes=256)
+                return keep.tile(shape, dtype, name=name, align_bytes=512)
             return stage.tile(shape, dtype, name=name, align_bytes=256, offset=offset)
 
         def round_h(e):

@@ -26,17 +26,15 @@ BANK_BYTES = 2048
 H_BANKS = 4
 LAST = E - 1
 
-WA_LOADS = (2, 3, 2, 2, 2, 1, 1, 1, 1, 1)
+WA_LOADS = (4, 3, 3, 2, 2, 1, 1)
 VECTOR_M = 80
 LAST_VECTOR_M = (84, 72)
-SCALAR_ALONE = 2
+SCALAR_ALONE = 0
 BEFORE_LAST = 2
-ROWS_FROM = 2
-ROW_PITCH = 256
+BLOCK_ROWS = 8
 
 AREA_BYTES = PACK * H * 4
 H_BYTES = C * PACK * 2
-Y_OFFSET = 2 * H_BYTES
 
 
 def tile_moe_elr_s_none_kernel(tc, x_words, x_scales, w_words, w_scales, wa, wb_words, wb_scales, offs, out):
@@ -48,19 +46,19 @@ def tile_moe_elr_s_none_kernel(tc, x_words, x_scales, w_words, w_scales, wa, wb_
         psum = ctx.enter_context(tc.psum_pool(name="psum", bufs=1))
 
         offsets = keep.tile([P, E * C // LIST_ROWS], U16, name="offsets", align_bytes=256)
-        x_table = keep.tile([P, T], I32, name="x_table", align_bytes=512)
-        x_plane = keep.tile([P, T], U8, name="x_plane", align_bytes=512)
-        pitched = keep.tile([P, E, ROW_PITCH], U8, name="planes", align_bytes=256)
-        planes = pitched[:, :, :N]
-        for plane in (x_plane[:], planes):
-            nc.vector.memset(plane.bitcast(I32), 0)
+        x_table = keep.tile([P, T], I32, name="x_table", align_bytes=256)
+        x_plane = keep.tile([P, T], U8, name="x_plane", align_bytes=256)
+        planes = keep.tile([P, 2, E, N], U8, name="planes", align_bytes=256)
+        for plane in (x_plane, planes):
+            nc.vector.memset(plane[:].bitcast(I32), 0)
+        plane_rows = planes[:].rearrange("p s e n -> p (s e n)").bitcast(I32)
 
         starts = [sum(WA_LOADS[:g]) for g in range(len(WA_LOADS))]
         raw, w_codes, wb_codes = {}, {}, {}
 
         def load_wa(g):
             first, count = starts[g], WA_LOADS[g]
-            tile = stage.tile([P, count, PACK * H], F32, name="raw%d" % first, align_bytes=512, offset=first * AREA_BYTES)
+            tile = stage.tile([P, count, PACK * H], F32, name="raw%d" % first, align_bytes=256, offset=first * AREA_BYTES)
             nc.sync.dma_start(out=tile[:], in_=wa[first : first + count].rearrange("e (p j) c -> p e (j c)", j=PACK))
             for u in range(count):
                 raw[first + u] = tile[:, u, :]
@@ -70,7 +68,7 @@ def tile_moe_elr_s_none_kernel(tc, x_words, x_scales, w_words, w_scales, wa, wb_
                 nc.sync.dma_start(out=plane[start + r : P : QUADRANT].bitcast(I32), in_=rows[r].bitcast(I32))
 
         def load_packed(codes, words, name, first, count):
-            tile = keep.tile([P, count, words.shape[2]], U8, name="%s%d" % (name, first), align_bytes=512)
+            tile = keep.tile([P, count, words.shape[2]], U8, name="%s%d" % (name, first), align_bytes=256)
             nc.sync.dma_start(out=tile[:].bitcast(I32), in_=words[:, first : first + count].bitcast(I32))
             for u in range(count):
                 codes[first + u] = tile[:, u, :]
@@ -78,20 +76,18 @@ def tile_moe_elr_s_none_kernel(tc, x_words, x_scales, w_words, w_scales, wa, wb_
         w_source = w_words[:, 0].rearrange("e p b -> p e b")
         wb_source = wb_words[:, 0].rearrange("e p n d -> p e (n d)")
         x_rows = x_scales[0].rearrange("(q r) t -> r q t", r=PLANE_ROWS)
-        w_rows = w_scales[:, 0].rearrange("e (q r) n -> r q e n", r=PLANE_ROWS)
-        wb_rows = wb_scales[:, 0].rearrange("e (q r) n -> r q e n", r=PLANE_ROWS)
 
         nc.sync.dma_start(out=x_table[:], in_=x_words[0].rearrange("p t d -> p (t d)").bitcast(I32))
         nc.sync.dma_start(offsets[:], offs)
-        load_wa(0)
         load_rows(x_plane[:], 0, x_rows, range(PLANE_ROWS))
-        for g in range(1, ROWS_FROM):
-            load_wa(g)
-        for r in range(PLANE_ROWS):
-            load_rows(planes, 0, w_rows, [r])
-            load_rows(planes, PLANE_ROWS, wb_rows, [r])
-            load_wa(ROWS_FROM + r)
-        for g in range(ROWS_FROM + PLANE_ROWS, len(WA_LOADS) - 1):
+        load_wa(0)
+        for which, scales in enumerate((w_scales, wb_scales)):
+            nc.sync.dma_start(out=planes[0:P:BLOCK_ROWS, which].bitcast(I32), in_=scales[:, 0].rearrange("e b n -> b e n").bitcast(I32))
+        load_wa(1)
+        load_wa(2)
+        for r in range(1, PLANE_ROWS):
+            nc.sync.dma_start(out=plane_rows[r:P:QUADRANT], in_=plane_rows[BLOCK_ROWS * r : P : QUADRANT])
+        for g in range(3, len(WA_LOADS) - 1):
             load_wa(g)
         load_packed(w_codes, w_source, "w_codes", 0, E)
         load_wa(len(WA_LOADS) - 1)
@@ -119,25 +115,27 @@ def tile_moe_elr_s_none_kernel(tc, x_words, x_scales, w_words, w_scales, wa, wb_
 
         def quantize_wa(e, t0, grouped, name):
             count = grouped.shape[1]
-            codes = ring.tile([P, count * P], U32, name="wa_codes" + name, align_bytes=256, bufs=1 if "q" in name else 5)
-            plane = ring.tile([P, count * P], U8, name="wa_plane" + name, align_bytes=256, bufs=1 if "q" in name else 5)
+            codes = ring.tile([P, count * P], U32, name="wa_codes" + name, align_bytes=256, bufs=1 if "q" in name else 4)
+            plane = ring.tile([P, count * P], U8, name="wa_plane" + name, align_bytes=256, bufs=1 if "q" in name else 4)
             nc.vector.quantize_mx(out=codes[:].bitcast(FP8X4), scales=plane[:], in_=grouped.rearrange("p u m j -> p (u m j)"))
             for u in range(count):
                 wa_codes[e, t0 + u] = codes[:, u * P : (u + 1) * P]
                 wa_plane[e, t0 + u] = plane[:, u * P : (u + 1) * P]
 
         def prepare_wa(e):
-            cut = 0 if e < SCALAR_ALONE else VECTOR_M
-            halves = [ring.tile([P, HALF, P, PACK], BF16, name="grouped%d" % half, align_bytes=256, bufs=5) for half in range(2)]
-            src = raw[e].rearrange("p (j i m h u) -> p h m j u i", j=2, i=2, h=2, u=HALF)
+            grouped = ring.tile([P, PACK, P, PACK], BF16, name="grouped", align_bytes=256, bufs=4)
+            src = raw[e].rearrange("p (j m t) -> p m j t", j=PACK, t=PACK)
+            share(grouped[:].rearrange("p t m j -> p m j t"), src, 0 if e < SCALAR_ALONE else VECTOR_M)
+            quantize_wa(e, 0, grouped[:], "whole")
+
+        def prepare_last_wa(e):
+            halves = [ring.tile([P, HALF, P, PACK], BF16, name="last%d" % half, align_bytes=256, bufs=1) for half in range(2)]
+            src = raw[e].rearrange("p (j m h u) -> p h m j u", j=PACK, h=2, u=HALF)
             for half, tile in enumerate(halves):
-                share(tile[:].rearrange("p u m (j i) -> p m j u i", i=2), src[:, half], LAST_VECTOR_M[half] if e == LAST else cut)
+                share(tile[:].rearrange("p u m j -> p m j u"), src[:, half], LAST_VECTOR_M[half])
             for half, tile in enumerate(halves):
-                if e < LAST:
-                    quantize_wa(e, HALF * half, tile[:], "h%d" % half)
-                else:
-                    for u in range(HALF):
-                        quantize_wa(e, HALF * half + u, tile[:, u : u + 1], "q%d" % (HALF * half + u))
+                for u in range(HALF):
+                    quantize_wa(e, HALF * half + u, tile[:, u : u + 1], "q%d" % (HALF * half + u))
 
         def first_product(e):
             slots = slice(e * C, (e + 1) * C)
@@ -155,7 +153,7 @@ def tile_moe_elr_s_none_kernel(tc, x_words, x_scales, w_words, w_scales, wa, wb_
 
         def held(shape, dtype, name, offset):
             if offset is None:
-                return keep.tile(shape, dtype, name=name, align_bytes=512)
+                return keep.tile(shape, dtype, name=name, align_bytes=256)
             return stage.tile(shape, dtype, name=name, align_bytes=256, offset=offset)
 
         def round_h(e):
@@ -181,7 +179,7 @@ def tile_moe_elr_s_none_kernel(tc, x_words, x_scales, w_words, w_scales, wa, wb_
                 nc.tensor.matmul_mx(
                     out=place[:, u, :],
                     lhsT=w_codes[first + u].bitcast(FP4X4),
-                    lhsT_scale=planes[:, first + u, :],
+                    lhsT_scale=planes[:, 0, first + u, :],
                     rhs=slot_words[:, slots].bitcast(FP8X4),
                     rhs_scale=slot_plane[:, slots],
                     start=opens and u == 0,
@@ -196,7 +194,7 @@ def tile_moe_elr_s_none_kernel(tc, x_words, x_scales, w_words, w_scales, wa, wb_
                 nc.tensor.matmul_mx(
                     out=place[:, u, :],
                     lhsT=wb_codes[e].bitcast(FP8X4),
-                    lhsT_scale=planes[PLANE_ROWS:, e, :],
+                    lhsT_scale=planes[:, 1, e, :],
                     rhs=h_codes[e][:].bitcast(FP8X4),
                     rhs_scale=h_plane[e][:],
                     start=opens and u == 0,
@@ -224,8 +222,10 @@ def tile_moe_elr_s_none_kernel(tc, x_words, x_scales, w_words, w_scales, wa, wb_
             store(firsts, copies)
 
         for i in range(E + 2):
-            if i < E:
+            if i < LAST:
                 prepare_wa(i)
+            if i == LAST:
+                prepare_last_wa(i)
             if i - 1 == LAST:
                 for group in stores[:BEFORE_LAST]:
                     finish(*group)

@@ -26,15 +26,22 @@ BANK_BYTES = 2048
 H_BANKS = 4
 LAST = E - 1
 
-WA_LOADS = (4, 3, 3, 2, 2, 1, 1)
+WA_LOADS = (2, 3, 2, 2, 2, 1, 1, 1, 1, 1)
 VECTOR_M = 80
-LAST_VECTOR_M = (84, 72)
-SCALAR_ALONE = 0
+LAST_PARTS = ((0, 32), (32, 128))
+LAST_VECTOR_M = ((20, 20), (64, 54))
+SCALAR_ALONE = 2
 BEFORE_LAST = 2
 BLOCK_ROWS = 8
+REUSED = {9: 0, 11: 3, 12: 4, 13: 6, 14: 8, 15: 1}
+RELEASED_BY = {9: 1, 11: 4, 12: 4, 13: 6, 14: 8, 15: 10}
+W_PLACE = 4096
+WB_PLACES = (3 * 8192 + 2048, 3 * 8192 + 4096, 3 * 8192 + 6144, 4 * 8192 + 2048)
+WB_RELEASED_BY = (11, 11, 11, 12)
 
 AREA_BYTES = PACK * H * 4
 H_BYTES = C * PACK * 2
+Y_OFFSET = 2 * H_BYTES
 
 
 def tile_moe_elr_s_none_kernel(tc, x_words, x_scales, w_words, w_scales, wa, wb_words, wb_scales, offs, out):
@@ -54,21 +61,29 @@ def tile_moe_elr_s_none_kernel(tc, x_words, x_scales, w_words, w_scales, wa, wb_
         plane_rows = planes[:].rearrange("p s e n -> p (s e n)").bitcast(I32)
 
         starts = [sum(WA_LOADS[:g]) for g in range(len(WA_LOADS))]
+        area = {first: first for first in starts}
+        area.update(REUSED)
         raw, w_codes, wb_codes = {}, {}, {}
 
         def load_wa(g):
             first, count = starts[g], WA_LOADS[g]
-            tile = stage.tile([P, count, PACK * H], F32, name="raw%d" % first, align_bytes=256, offset=first * AREA_BYTES)
+            tile = stage.tile([P, count, PACK * H], F32, name="raw%d" % first, align_bytes=256, offset=area[first] * AREA_BYTES)
             nc.sync.dma_start(out=tile[:], in_=wa[first : first + count].rearrange("e (p j) c -> p e (j c)", j=PACK))
             for u in range(count):
                 raw[first + u] = tile[:, u, :]
+
+        def load_last_part(part):
+            m0, m1 = LAST_PARTS[part]
+            tile = stage.tile([P, PACK, PACK * (m1 - m0)], F32, name="raw_last%d" % part, align_bytes=256, offset=area[LAST] * AREA_BYTES + m0 * PACK * PACK * 4)
+            nc.sync.dma_start(out=tile[:], in_=wa[LAST, :, PACK * m0 : PACK * m1].rearrange("(p j) c -> p j c", j=PACK))
+            raw[LAST, part] = tile[:]
 
         def load_rows(plane, start, rows, which):
             for r in which:
                 nc.sync.dma_start(out=plane[start + r : P : QUADRANT].bitcast(I32), in_=rows[r].bitcast(I32))
 
-        def load_packed(codes, words, name, first, count):
-            tile = keep.tile([P, count, words.shape[2]], U8, name="%s%d" % (name, first), align_bytes=256)
+        def load_packed(codes, words, name, first, count, offset):
+            tile = stage.tile([P, count, words.shape[2]], U8, name="%s%d" % (name, first), align_bytes=256, offset=offset)
             nc.sync.dma_start(out=tile[:].bitcast(I32), in_=words[:, first : first + count].bitcast(I32))
             for u in range(count):
                 codes[first + u] = tile[:, u, :]
@@ -79,20 +94,15 @@ def tile_moe_elr_s_none_kernel(tc, x_words, x_scales, w_words, w_scales, wa, wb_
 
         nc.sync.dma_start(out=x_table[:], in_=x_words[0].rearrange("p t d -> p (t d)").bitcast(I32))
         nc.sync.dma_start(offsets[:], offs)
-        load_rows(x_plane[:], 0, x_rows, range(PLANE_ROWS))
         load_wa(0)
+        load_rows(x_plane[:], 0, x_rows, range(PLANE_ROWS))
         for which, scales in enumerate((w_scales, wb_scales)):
             nc.sync.dma_start(out=planes[0:P:BLOCK_ROWS, which].bitcast(I32), in_=scales[:, 0].rearrange("e b n -> b e n").bitcast(I32))
-        load_wa(1)
-        load_wa(2)
+        for g in range(1, len(WA_LOADS)):
+            if starts[g] not in REUSED:
+                load_wa(g)
         for r in range(1, PLANE_ROWS):
             nc.sync.dma_start(out=plane_rows[r:P:QUADRANT], in_=plane_rows[BLOCK_ROWS * r : P : QUADRANT])
-        for g in range(3, len(WA_LOADS) - 1):
-            load_wa(g)
-        load_packed(w_codes, w_source, "w_codes", 0, E)
-        load_wa(len(WA_LOADS) - 1)
-        for first in range(0, E, GROUP):
-            load_packed(wb_codes, wb_source, "wb_codes", first, GROUP)
 
         slot_words = keep.tile([P, E * C], U32, name="slot_words", align_bytes=256)
         slot_plane = keep.tile([P, E * C], U8, name="slot_plane", align_bytes=256)
@@ -115,27 +125,33 @@ def tile_moe_elr_s_none_kernel(tc, x_words, x_scales, w_words, w_scales, wa, wb_
 
         def quantize_wa(e, t0, grouped, name):
             count = grouped.shape[1]
-            codes = ring.tile([P, count * P], U32, name="wa_codes" + name, align_bytes=256, bufs=1 if "q" in name else 4)
-            plane = ring.tile([P, count * P], U8, name="wa_plane" + name, align_bytes=256, bufs=1 if "q" in name else 4)
+            codes = ring.tile([P, count * P], U32, name="wa_codes" + name, align_bytes=256, bufs=1 if "q" in name else 5)
+            plane = ring.tile([P, count * P], U8, name="wa_plane" + name, align_bytes=256, bufs=1 if "q" in name else 5)
             nc.vector.quantize_mx(out=codes[:].bitcast(FP8X4), scales=plane[:], in_=grouped.rearrange("p u m j -> p (u m j)"))
             for u in range(count):
                 wa_codes[e, t0 + u] = codes[:, u * P : (u + 1) * P]
                 wa_plane[e, t0 + u] = plane[:, u * P : (u + 1) * P]
 
         def prepare_wa(e):
-            grouped = ring.tile([P, PACK, P, PACK], BF16, name="grouped", align_bytes=256, bufs=4)
-            src = raw[e].rearrange("p (j m t) -> p m j t", j=PACK, t=PACK)
-            share(grouped[:].rearrange("p t m j -> p m j t"), src, 0 if e < SCALAR_ALONE else VECTOR_M)
-            quantize_wa(e, 0, grouped[:], "whole")
+            cut = 0 if e < SCALAR_ALONE else VECTOR_M
+            halves = [ring.tile([P, HALF, P, PACK], BF16, name="grouped%d" % half, align_bytes=256, bufs=5) for half in range(2)]
+            src = raw[e].rearrange("p (j i m h u) -> p h m j u i", j=2, i=2, h=2, u=HALF)
+            for half, tile in enumerate(halves):
+                share(tile[:].rearrange("p u m (j i) -> p m j u i", i=2), src[:, half], cut)
+            for half, tile in enumerate(halves):
+                quantize_wa(e, HALF * half, tile[:], "h%d" % half)
 
-        def prepare_last_wa(e):
-            halves = [ring.tile([P, HALF, P, PACK], BF16, name="last%d" % half, align_bytes=256, bufs=1) for half in range(2)]
-            src = raw[e].rearrange("p (j m h u) -> p h m j u", j=PACK, h=2, u=HALF)
-            for half, tile in enumerate(halves):
-                share(tile[:].rearrange("p u m j -> p m j u"), src[:, half], LAST_VECTOR_M[half])
-            for half, tile in enumerate(halves):
+        def round_last(part):
+            m0, m1 = LAST_PARTS[part]
+            src = raw[LAST, part].rearrange("p (j i) (m h u) -> p h m j u i", i=2, h=2, u=HALF)
+            for half, tile in enumerate(last_halves):
+                dst = tile[:, :, m0:m1].rearrange("p u m (j i) -> p m j u i", i=2)
+                share(dst, src[:, half], LAST_VECTOR_M[part][half])
+
+        def quantize_last():
+            for half, tile in enumerate(last_halves):
                 for u in range(HALF):
-                    quantize_wa(e, HALF * half + u, tile[:, u : u + 1], "q%d" % (HALF * half + u))
+                    quantize_wa(LAST, HALF * half + u, tile[:, u : u + 1], "q%d" % (HALF * half + u))
 
         def first_product(e):
             slots = slice(e * C, (e + 1) * C)
@@ -157,12 +173,17 @@ def tile_moe_elr_s_none_kernel(tc, x_words, x_scales, w_words, w_scales, wa, wb_
             return stage.tile(shape, dtype, name=name, align_bytes=256, offset=offset)
 
         def round_h(e):
-            h_bf16[e] = held([P, C, PACK], BF16, "h_bf16_%d" % e, (e + 1) * AREA_BYTES if e + 1 in starts[:-1] else None)
+            h_bf16[e] = held([P, C, PACK], BF16, "h_bf16_%d" % e, area[e + 1] * AREA_BYTES if e + 1 in starts[:-1] else None)
             copy = nc.scalar.copy if e < LAST else nc.vector.tensor_copy
             copy(out=h_bf16[e][:], in_=h_banks[e].rearrange("p t n -> p n t"))
 
+        def codes_place(e):
+            if e == LAST - 1:
+                return area[LAST] * AREA_BYTES + AREA_BYTES // 2
+            return area[e + 2] * AREA_BYTES + H_BYTES if e + 2 in starts[:-1] else None
+
         def quantize_h(e):
-            h_codes[e] = held([P, C], U32, "h_codes%d" % e, min(e + 2, LAST) * AREA_BYTES + H_BYTES if e + 2 in starts[:-1] or e == LAST - 1 else None)
+            h_codes[e] = held([P, C], U32, "h_codes%d" % e, codes_place(e))
             h_plane[e] = keep.tile([P, C], U8, name="h_plane%d" % e, align_bytes=256)
             nc.vector.quantize_mx(
                 out=h_codes[e][:].bitcast(FP8X4), scales=h_plane[e][:], in_=h_bf16[e][:].rearrange("p n t -> p (n t)")
@@ -216,16 +237,36 @@ def tile_moe_elr_s_none_kernel(tc, x_words, x_scales, w_words, w_scales, wa, wb_
             ([12, 15], [nc.vector.tensor_copy, nc.vector.tensor_copy]),
         )
 
+        late_groups = {10: (2, 1), 12: (3, 0)}
+
         def finish(firsts, copies):
             for first in firsts:
-                second_products(first, False, True)
+                if first in late_groups:
+                    open_y(first, *late_groups[first])
+                    second_products(first, True, False)
+                    frozen_products(first, False, True)
+                else:
+                    second_products(first, False, True)
             store(firsts, copies)
 
+        last_halves = [keep.tile([P, HALF, P, PACK], BF16, name="last%d" % half, align_bytes=256) for half in range(2)]
         for i in range(E + 2):
             if i < LAST:
                 prepare_wa(i)
             if i == LAST:
-                prepare_last_wa(i)
+                round_last(0)
+                round_last(1)
+                quantize_last()
+            for first, by in RELEASED_BY.items():
+                if by == i and first < LAST:
+                    load_wa(starts.index(first))
+            if i == RELEASED_BY[LAST]:
+                load_last_part(0)
+                load_packed(w_codes, w_source, "w_codes", 0, E, W_PLACE)
+                load_last_part(1)
+            for g, by in enumerate(WB_RELEASED_BY):
+                if by == i:
+                    load_packed(wb_codes, wb_source, "wb_codes", g * GROUP, GROUP, WB_PLACES[g])
             if i - 1 == LAST:
                 for group in stores[:BEFORE_LAST]:
                     finish(*group)
@@ -235,7 +276,7 @@ def tile_moe_elr_s_none_kernel(tc, x_words, x_scales, w_words, w_scales, wa, wb_
             if 0 <= i - 2:
                 quantize_h(i - 2)
             if i - 1 == LAST - 1:
-                for first, count, index in ((0, 4, 4), (4, 2, 5), (6, 2, 6), (8, 2, 7), (12, 3, 0), (10, 2, 1), (15, 1, 2)):
+                for first, count, index in ((0, 4, 4), (4, 2, 5), (6, 2, 6), (8, 2, 7), (15, 1, 2)):
                     open_y(first, count, index)
                     frozen_products(first, True, False)
         for group in stores[BEFORE_LAST:]:

from contextlib import ExitStack

import concourse.mybir as mybir

K, T, E, C, H, N = 512, 512, 16, 128, 512, 128
FLOPS = 2 * E * C * (K * H + K * N + H * N)

F32 = mybir.dt.float32
BF16 = mybir.dt.bfloat16
I32 = mybir.dt.int32
U32 = mybir.dt.uint32
U16 = mybir.dt.uint16
U8 = mybir.dt.uint8
FP8X4 = mybir.dt.float8_e4m3fn_x4
FP4X4 = mybir.dt.float4_e2m1fn_x4

P = 128
PACK = 4
HALF = PACK // 2
PLANE_ROWS = 4
QUADRANT = 32
LIST_ROWS = 16
GATHER = 384
GROUP = 4
BANK_BYTES = 2048
H_BANKS = 4
LAST = E - 1

WA_LOADS = (2, 3, 2, 2, 2, 1, 1, 1, 1, 1)
VECTOR_M = 80
LAST_PARTS = ((0, 32), (32, 128))
LAST_VECTOR_M = ((20, 20), (64, 54))
SCALAR_ALONE = 2
BEFORE_LAST = 2
BLOCK_ROWS = 8
REUSED = {9: 0, 11: 3, 12: 4, 13: 6, 14: 8, 15: 1}
RELEASED_BY = {9: 1, 11: 4, 12: 4, 13: 6, 14: 8, 15: 10}
W_PLACE = 4096
WB_PLACES = (3 * 8192 + 2048, 3 * 8192 + 4096, 3 * 8192 + 6144, 4 * 8192 + 2048)
WB_RELEASED_BY = (11, 11, 11, 12)

AREA_BYTES = PACK * H * 4
H_BYTES = C * PACK * 2
Y_OFFSET = 2 * H_BYTES


def tile_moe_elr_s_none_kernel(tc, x_words, x_scales, w_words, w_scales, wa, wb_words, wb_scales, offs, out):
    nc = tc.nc
    with ExitStack() as ctx:
        keep = ctx.enter_context(tc.tile_pool(name="keep", bufs=1))
        ring = ctx.enter_context(tc.tile_pool(name="ring", bufs=6))
        stage = ctx.enter_context(tc.tile_pool(name="stage", bufs=1))
        psum = ctx.enter_context(tc.psum_pool(name="psum", bufs=1))

        offsets = keep.tile([P, E * C // LIST_ROWS], U16, name="offsets", align_bytes=256)
        x_table = keep.tile([P, T], I32, name="x_table", align_bytes=256)
        x_plane = keep.tile([P, T], U8, name="x_plane", align_bytes=256)
        planes = keep.tile([P, 2, E, N], U8, name="planes", align_bytes=256)
        for plane in (x_plane, planes):
            nc.vector.memset(plane[:].bitcast(I32), 0)
        plane_rows = planes[:].rearrange("p s e n -> p (s e n)").bitcast(I32)

        starts = [sum(WA_LOADS[:g]) for g in range(len(WA_LOADS))]
        area = {first: first for first in starts}
        area.update(REUSED)
        raw, w_codes, wb_codes = {}, {}, {}

        def load_wa(g):
            first, count = starts[g], WA_LOADS[g]
            tile = stage.tile([P, count, PACK * H], F32, name="raw%d" % first, align_bytes=256, offset=area[first] * AREA_BYTES)
            nc.sync.dma_start(out=tile[:], in_=wa[first : first + count].rearrange("e (p j) c -> p e (j c)", j=PACK))
            for u in range(count):
                raw[first + u] = tile[:, u, :]

        def load_last_part(part):
            m0, m1 = LAST_PARTS[part]
            tile = stage.tile([P, PACK, PACK * (m1 - m0)], F32, name="raw_last%d" % part, align_bytes=256, offset=area[LAST] * AREA_BYTES + m0 * PACK * PACK * 4)
            nc.sync.dma_start(out=tile[:], in_=wa[LAST, :, PACK * m0 : PACK * m1].rearrange("(p j) c -> p j c", j=PACK))
            raw[LAST, part] = tile[:]

        def load_rows(plane, start, rows, which):
            for r in which:
                nc.sync.dma_start(out=plane[start + r : P : QUADRANT].bitcast(I32), in_=rows[r].bitcast(I32))

        def load_packed(codes, words, name, first, count, offset):
            tile = stage.tile([P, count, words.shape[2]], U8, name="%s%d" % (name, first), align_bytes=256, offset=offset)
            nc.sync.dma_start(out=tile[:].bitcast(I32), in_=words[:, first : first + count].bitcast(I32))
            for u in range(count):
                codes[first + u] = tile[:, u, :]

        w_source = w_words[:, 0].rearrange("e p b -> p e b")
        wb_source = wb_words[:, 0].rearrange("e p n d -> p e (n d)")
        x_rows = x_scales[0].rearrange("(q r) t -> r q t", r=PLANE_ROWS)

        nc.sync.dma_start(out=x_table[:], in_=x_words[0].rearrange("p t d -> p (t d)").bitcast(I32))
        nc.sync.dma_start(offsets[:], offs)
        load_wa(0)
        load_rows(x_plane[:], 0, x_rows, range(PLANE_ROWS))
        for which, scales in enumerate((w_scales, wb_scales)):
            nc.sync.dma_start(out=planes[0:P:BLOCK_ROWS, which].bitcast(I32), in_=scales[:, 0].rearrange("e b n -> b e n").bitcast(I32))
        for g in range(1, len(WA_LOADS)):
            if starts[g] not in REUSED:
                load_wa(g)
        for r in range(1, PLANE_ROWS):
            nc.sync.dma_start(out=plane_rows[r:P:QUADRANT], in_=plane_rows[BLOCK_ROWS * r : P : QUADRANT])

        slot_words = keep.tile([P, E * C], U32, name="slot_words", align_bytes=256)
        slot_plane = keep.tile([P, E * C], U8, name="slot_plane", align_bytes=256)
        for s0 in range(0, E * C, GATHER):
            s1 = min(s0 + GATHER, E * C)
            piece = offsets[:, s0 // LIST_ROWS : s1 // LIST_ROWS]
            nc.vector.tensor_copy(slot_words[:, s0:s1], x_table[:].bitcast(U32).indirect(piece))
            nc.vector.tensor_copy(slot_plane[:, s0:s1], x_plane[:].indirect(piece))

        wa_codes, wa_plane, h_banks, h_bf16, h_codes, h_plane, y_place = {}, {}, {}, {}, {}, {}, {}

        def bank(name, index, count=PACK):
            tile = psum.tile([P, count, C], F32, name=name, offset=index * BANK_BYTES)
            return tile[:]

        def share(dst, src, cut):
            if cut:
                nc.vector.tensor_copy(out=dst[:, :cut], in_=src[:, :cut])
            nc.scalar.copy(out=dst[:, cut:], in_=src[:, cut:])

        def quantize_wa(e, t0, grouped, name):
            count = grouped.shape[1]
            codes = ring.tile([P, count * P], U32, name="wa_codes" + name, align_bytes=256, bufs=1 if "q" in name else 5)
            plane = ring.tile([P, count * P], U8, name="wa_plane" + name, align_bytes=256, bufs=1 if "q" in name else 5)
            nc.vector.quantize_mx(out=codes[:].bitcast(FP8X4), scales=plane[:], in_=grouped.rearrange("p u m j -> p (u m j)"))
            for u in range(count):
                wa_codes[e, t0 + u] = codes[:, u * P : (u + 1) * P]
                wa_plane[e, t0 + u] = plane[:, u * P : (u + 1) * P]

        def prepare_wa(e):
            cut = 0 if e < SCALAR_ALONE else VECTOR_M
            halves = [ring.tile([P, HALF, P, PACK], BF16, name="grouped%d" % half, align_bytes=256, bufs=5) for half in range(2)]
            src = raw[e].rearrange("p (j i m h u) -> p h m j u i", j=2, i=2, h=2, u=HALF)
            for half, tile in enumerate(halves):
                share(tile[:].rearrange("p u m (j i) -> p m j u i", i=2), src[:, half], cut)
            for half, tile in enumerate(halves):
                quantize_wa(e, HALF * half, tile[:], "h%d" % half)

        def round_last(part):
            m0, m1 = LAST_PARTS[part]
            src = raw[LAST, part].rearrange("p (j i) (m h u) -> p h m j u i", i=2, h=2, u=HALF)
            for half, tile in enumerate(last_halves):
                dst = tile[:, :, m0:m1].rearrange("p u m (j i) -> p m j u i", i=2)
                share(dst, src[:, half], LAST_VECTOR_M[part][half])

        def quantize_last():
            for half, tile in enumerate(last_halves):
                for u in range(HALF):
                    quantize_wa(LAST, HALF * half + u, tile[:, u : u + 1], "q%d" % (HALF * half + u))

        def first_product(e):
            slots = slice(e * C, (e + 1) * C)
            h_banks[e] = bank("h%d" % e, e % H_BANKS)
            for t in range(PACK):
                nc.tensor.matmul_mx(
                    out=h_banks[e][:, t, :],
                    lhsT=wa_codes[e, t].bitcast(FP8X4),
                    lhsT_scale=wa_plane[e, t],
                    rhs=slot_words[:, slots].bitcast(FP8X4),
                    rhs_scale=slot_plane[:, slots],
                    start=True,
                    stop=True,
                )

        def held(shape, dtype, name, offset):
            if offset is None:
                return keep.tile(shape, dtype, name=name, align_bytes=256)
            return stage.tile(shape, dtype, name=name, align_bytes=256, offset=offset)

        def round_h(e):
            h_bf16[e] = held([P, C, PACK], BF16, "h_bf16_%d" % e, area[e + 1] * AREA_BYTES if e + 1 in starts[:-1] else None)
            copy = nc.scalar.copy if e < LAST else nc.vector.tensor_copy
            copy(out=h_bf16[e][:], in_=h_banks[e].rearrange("p t n -> p n t"))

        def codes_place(e):
            if e == LAST - 1:
                return area[LAST] * AREA_BYTES + AREA_BYTES // 2
            return area[e + 2] * AREA_BYTES + H_BYTES if e + 2 in starts[:-1] else None

        def quantize_h(e):
            h_codes[e] = held([P, C], U32, "h_codes%d" % e, codes_place(e))
            h_plane[e] = keep.tile([P, C], U8, name="h_plane%d" % e, align_bytes=256)
            nc.vector.quantize_mx(
                out=h_codes[e][:].bitcast(FP8X4), scales=h_plane[e][:], in_=h_bf16[e][:].rearrange("p n t -> p (n t)")
            )

        def open_y(first, count, index):
            y_place[first] = bank("y%d" % first, index, count)

        def frozen_products(first, opens, closes):
            place = y_place[first]
            count = place.shape[1]
            for u in range(count):
                slots = slice((first + u) * C, (first + u + 1) * C)
                nc.tensor.matmul_mx(
                    out=place[:, u, :],
                    lhsT=w_codes[first + u].bitcast(FP4X4),
                    lhsT_scale=planes[:, 0, first + u, :],
                    rhs=slot_words[:, slots].bitcast(FP8X4),
                    rhs_scale=slot_plane[:, slots],
                    start=opens and u == 0,
                    stop=closes and u == count - 1,
                )

        def second_products(first, opens, closes):
            place = y_place[first]
            count = place.shape[1]
            for u in range(count):
                e = first + u
                nc.tensor.matmul_mx(
                    out=place[:, u, :],
                    lhsT=wb_codes[e].bitcast(FP8X4),
                    lhsT_scale=planes[:, 1, e, :],
                    rhs=h_codes[e][:].bitcast(FP8X4),
                    rhs_scale=h_plane[e][:],
                    start=opens and u == 0,
                    stop=closes and u == count - 1,
                )

        def store(firsts, copies, offset=None):
            width = sum(y_place[first].shape[1] for first in firsts)
            y = held([P, width, C], F32, "y_out%d" % firsts[0], offset)
            for first, copy in zip(firsts, copies):
                place = y_place[first]
                copy(out=y[:, first - firsts[0] : first - firsts[0] + place.shape[1]], in_=place)
            nc.sync.dma_start(out=out[:, firsts[0] * C : (firsts[0] + width) * C], in_=y[:].rearrange("p u n -> p (u n)"))

        stores = (
            ([0], [nc.scalar.copy]),
            ([4, 6], [nc.scalar.copy, nc.scalar.copy]),
            ([8, 10], [nc.scalar.copy, nc.scalar.copy]),
            ([12, 15], [nc.vector.tensor_copy, nc.vector.tensor_copy]),
        )

        late_groups = {10: (2, 1), 12: (3, 0)}

        def finish(firsts, copies):
            for first in firsts:
                if first in late_groups:
                    open_y(first, *late_groups[first])
                    second_products(first, True, False)
                    frozen_products(first, False, True)
                else:
                    second_products(first, False, True)
            store(firsts, copies)

        last_halves = [keep.tile([P, HALF, P, PACK], BF16, name="last%d" % half, align_bytes=256) for half in range(2)]
        for i in range(E + 2):
            if i < LAST:
                prepare_wa(i)
            if i == LAST:
                round_last(0)
                round_last(1)
                quantize_last()
            for first, by in RELEASED_BY.items():
                if by == i and first < LAST:
                    load_wa(starts.index(first))
            if i == RELEASED_BY[LAST]:
                load_last_part(0)
                load_packed(w_codes, w_source, "w_codes", 0, E, W_PLACE)
                load_last_part(1)
            for g, by in enumerate(WB_RELEASED_BY):
                if by == i:
                    load_packed(wb_codes, wb_source, "wb_codes", g * GROUP, GROUP, WB_PLACES[g])
            if i - 1 == LAST:
                for group in stores[:BEFORE_LAST]:
                    finish(*group)
            if 0 <= i - 1 <= LAST:
                first_product(i - 1)
                round_h(i - 1)
            if 0 <= i - 2:
                quantize_h(i - 2)
            if i - 1 == LAST - 1:
                for first, count, index in ((0, 4, 4), (4, 2, 5), (6, 2, 6), (8, 2, 7), (15, 1, 2)):
                    open_y(first, count, index)
                    frozen_products(first, True, False)
        for group in stores[BEFORE_LAST:]:
            finish(*group)
